import numpy as np, ml_dtypes
CORES = [16,17,18,19,32,33,34,35]
N = 8
BF = ml_dtypes.bfloat16
def f(rng, *shape):
    return (rng.standard_normal(shape, dtype=np.float32) * np.exp2(rng.integers(-2, 3, shape[:-1] + (1,)))).astype(BF)
def wide(rng, *shape):
    v = f(rng, *shape).astype(np.float32); k = shape[:-2] + (1, shape[-1])
    return (v * np.exp2(rng.integers(-6, 7, k)) * (rng.random(k) > 0.0625)).astype(BF)
def gentries(a):
    return np.ascontiguousarray(a.reshape(8, 16, -1).transpose(0, 2, 1)).reshape(8, -1)
def gtable(e):
    e = np.asarray(e); return np.ascontiguousarray(e.reshape(8, -1, 16).transpose(0, 2, 1)).reshape(128, -1).astype(np.int32)
P, E, S, W, TT, CAPP = 2, 768, 4096, 256, 2048, 128
I, LS = N * S, 12
def events(x):
    return np.stack([gentries(u) for u in x]).reshape(N, 8, P, E).transpose(0, 2, 1, 3).astype(np.int64)
def unevents(e):
    return np.stack([gtable(u) for u in e.transpose(0, 2, 1, 3).reshape(N, 8, P * E)])
def shifts(sh, t):
    return np.take_along_axis(sh.astype(np.int64).reshape(N, 8, P, TT).transpose(0, 2, 1, 3), t, -1)
def evenly(rng):
    c = rng.multinomial(E, np.full(N, 2.0 ** -3), (P, 8, N)); x = np.sum(np.maximum(c - CAPP, 0), -1); c = np.minimum(c, CAPP)
    while x.any():
        i = np.argmin(c, -1)[..., None]; np.put_along_axis(c, i, np.take_along_axis(c, i, -1) + (x > 0)[..., None], -1); x = x - (x > 0)
    return c
def fully(rng):
    a = np.array(([CAPP] * (E // CAPP) + [E % CAPP] + [0] * N)[:N]); o = np.argsort(rng.random((P, 8, N, N)), -1)
    o[1::2] = o[1::2, :, :1].copy()
    return a[o]
def draw(rng, cnt, t, sh, v, crowd=False):
    pl = np.zeros((N, P, 8, E), np.int64)
    for k in range(P):
        for g in range(8):
            got = [[] for r in range(N)]
            for q in range(N):
                m = int(np.sum(cnt[k, g, :, q])); h = m // 2
                s = rng.permutation(np.append(np.arange(m - h), np.arange(S - h, S))) if crowd else rng.permutation(S)[:m]
                for r, u in enumerate(np.split(s, np.add.accumulate(cnt[k, g, :, q])[:-1])): got[r].append(u + S * q)
            for r in range(N): pl[r, k, g] = rng.permutation(np.concatenate(got[r]))
    v = v.astype(np.float32) * (1 + rng.random((N, 128, S), dtype=np.float32))
    rate = ((1 + rng.random((N, 128, 1))) * np.exp2(-rng.integers(7, 14, (N, 128, 1)))).astype(np.float32)
    return {"v": v, "last": rng.integers(-4096, 1, (N, 8, S)).astype(np.int32), "rate": rate, "sh": sh.astype(np.int32),
            "pix": unevents((pl - shifts(sh, t)) & (I - 1)), "tm": unevents(t), "pol": unevents(2 * rng.integers(0, 2, (N, P, 8, E)) - 1)}
def setup_inputs(rng):
    return draw(rng, evenly(rng), rng.integers(0, TT, (N, P, 8, E)), rng.integers(0, I, (N, 8, P * TT)), f(rng, N, 128, S))
def setup_inputs_full(rng):
    return draw(rng, fully(rng), rng.integers(0, TT, (N, P, 8, E)), rng.integers(0, I, (N, 8, P * TT)), f(rng, N, 128, S))
def setup_inputs_ends(rng):
    t = np.array([0, 1, TT - 1])[rng.integers(0, 3, (N, P, 8, E))]
    d = draw(rng, evenly(rng), t, rng.integers(0, I, (N, 8, P * TT)), f(rng, N, 128, S), True)
    d["last"] = (-4096 * rng.integers(0, 2, (N, 8, S))).astype(np.int32); return d
def setup_inputs_still(rng):
    t = np.repeat(rng.integers(0, TT, (N, P, 8, 1)), E, -1); sh = rng.integers(0, I, (N, 8, P * TT)); sh[rng.permutation(N)[:2]] = 0
    return draw(rng, evenly(rng), t, sh, f(rng, N, 128, S))
def setup_inputs_spread(rng):
    return draw(rng, evenly(rng), rng.integers(0, TT, (N, P, 8, E)), rng.integers(0, I, (N, 8, P * TT)), wide(rng, N, 128, S))
def check_inputs(d):
    bad = [] if np.isfinite(d["v"]).all() else ["v finite"]
    for a, lo, hi in (("rate", 2.0 ** -14, 2.0 ** -6), ("last", -4096, 0), ("sh", 0, I - 1), ("pix", 0, I - 1), ("tm", 0, TT - 1)):
        if not ((d[a] >= lo) & (d[a] <= hi)).all(): bad.append(a + " range")
    if not ((d["pol"] == 1) | (d["pol"] == -1)).all(): bad.append("pol is 1 or -1")
    if bad: return bad
    pl = (events(d["pix"]) + shifts(d["sh"], events(d["tm"]))) & (I - 1)
    r, k, g = np.arange(N)[:, None, None, None], np.arange(P)[None, :, None, None], np.arange(8)[None, None, :, None]
    if np.bincount(((((r * P + k) * 8 + g) * N) + (pl >> LS)).reshape(-1)).max() > CAPP: bad.append("CAPP")
    if np.unique((k * 8 + g) * I + pl).size != pl.size: bad.append("places of a packet differ")
    return bad
def reference(v, last, rate, sh, pix, tm, pol):
    V = v.astype(np.float64).reshape(N, 8, 16, S); L = last.astype(np.int64); a = rate.astype(np.float64).reshape(N, 8, 16)
    t, w = events(tm), events(pol); pl = (events(pix) + shifts(sh, t)) & (I - 1)
    y = np.zeros((N, 8, 16, P, E), np.float64); g = np.arange(8)[None, :, None]
    for k in range(P):
        q, c, now = pl[:, k] >> LS, pl[:, k] & (S - 1), TT * k + t[:, k]
        V[q, g, :, c] = V[q, g, :, c] * np.exp(-a[q, g] * (now - L[q, g, c])[..., None]) + w[:, k][..., None]
        L[q, g, c] = now
        s = np.zeros((N, 8, E, 16))
        for e in (-1, 1, -W, W): s = s + V[q, g, :, np.minimum(np.maximum(c + e, 0), S - 1)]
        y[:, :, :, k] = s.transpose(0, 1, 3, 2)
    return {"y": y.reshape(N, 128, P * E).astype(np.float32)}

@@ -1,0 +1,446 @@
+from concourse.bass import DstId, RemoteDMATransfer
+from concourse.mybir import AluOpType as A, ActivationFunctionType as F
+
+NC = 64
+E, CAP, S = 768, 128, 4096
+OFFC = 2560
+
+I32, F32, BF, U16, F16 = "int32", "float32", "bfloat16", "uint16", "float16"
+_SB = {
+    I32: dict(tm_i=96, pix_i=96, pol_i=96, shI=512, last_i=256, k16=16, k15=16, parI=1, colI=48, hiI=96, loI=96,
+              u=96, q=96, c=96, xi=128, ci=128, ti=128, pi=128),
+    F32: dict(rate_s=1, V=5120, L=5120, W=2048, t16=16, tbl=8, pcol=1, par=1, dmask=768, negf=128, onef=128, nB1=128,
+              nB=128, idf=128, Zf=144, nrate=1, lf=256, win=512, mask=1536, ta=96, tb=96, tp=96, c4=96, pay=96,
+              gexp=1536, psend=128, pland=128, Lg=2048, Ex=2048, wr=2048, prod=2048, A0=1024, N1=2048, N3=2048,
+              N4=2048, acc=2048, OUT=2048, ans=2048, Y=1536, rel=256),
+    BF: dict(ones=512, big=2048, negb=128, B1=128, B=128, U1=128, U=128, ident=128, Zb=144, Rep=2048, reset=384,
+             C0=128, C1=128, hs=512, cand=1536, qb=96, ind=768, scn=768, M=768, wb=128),
+    U16: dict(colU=48, pmU=48, hiU=96, loU=96, slot=96, cg=128, cs=128, n1=128, n2=128, n3=128, n4=128),
+    F16: dict(th=128)}
+SCRATCH = {n: ("sbuf", [128, w], d) for d, ws in _SB.items() for n, w in ws.items()}
+for _b in range(8):
+    SCRATCH["P%d" % _b] = ("psum", [128, 512], F32)
+SEMAPHORES = ["cv", "ca", "cp", "cq", "sent", "pay0", "pay1", "ans0", "ans1", "rel0", "rel1"] + \
+             ["d%d" % i for i in range(16)]
+
+CHUNKS = [[(0, 2, "v"), (2, 4, "v"), (7, 8, "v"), (4, 7, "p")],
+          [(0, 1, "v"), (1, 2, "v"), (2, 4, "v"), (6, 7, "v"), (7, 8, "v"), (4, 6, "p")]]
+
+
+def cs_(a, n):
+    return slice(a, a + n)
+
+
+def layout(T, topo):
+    cores = list(T.cores)
+    order, helper, used = {}, {}, set(cores)
+    for o, co in enumerate(cores):
+        near = [r for r, c in enumerate(cores) if topo.chip(c) == topo.chip(co)]
+        far = [r for r in range(len(cores)) if r not in near]
+        i = near.index(o)
+        order[o] = [far[(i + j) % len(far)] for j in range(len(far))] + \
+                   [near[(i + j) % len(near)] for j in range(1, len(near) + 1)]
+        helper[o] = []
+        for j in range(2):
+            d = cores[order[o][j]]
+            cand = [h for h in range(NC) if h not in used and topo.mates(topo.chip(h), topo.chip(d))
+                    and (topo.die(h) == topo.die(co)) == (j == 1) and topo.may_write(co, h) and topo.may_write(h, d)]
+            if not cand:
+                cand = [h for h in topo.cores_of(co) if h not in used and topo.die(h) != topo.die(co)]
+            helper[o].append(cand[0])
+            used.add(cand[0])
+    return order, helper
+
+
+def transfer(topo, d, es, sem, src, dst):
+    a = topo.addr(d)
+    return RemoteDMATransfer(dst_ids=[DstId(rid=a[0], pnc=a[1])], dma_engine_mask=sum(1 << e for e in es),
+                             remote_sem=sem, src=src, dst=dst)
+
+
+def helper_program(g, core, T, topo, o, d):
+    es = topo.engines(core, d)
+    for k in range(2):
+        g.wait_ge(T.sem["rel%d" % k], 8)
+        g.remote_dma_fused([transfer(topo, d, es, T.sem["ans%d" % k], T.rel[:, cs_(128 * k, 128)],
+                                     T.ans[:, cs_(1024 * k + 128 * o, 128)])], local_sem=T.sem.sent)
+    g.wait_ge(T.sem.sent, 2 * len(es))
+
+
+def rank_program(g, core, T, topo):
+    order, helper = layout(T, topo)
+    me = T.rank_of(core)
+    cores = list(T.cores)
+    if me is None:
+        for o, hs in helper.items():
+            if core in hs:
+                helper_program(g, core, T, topo, o, cores[order[o][hs.index(core)]])
+        return
+    Q = {"v": g.vector, "a": g.scalar, "p": g.tensor, "g": g, "s": g.sync}
+    CS = {"v": "cv", "a": "ca", "p": "cp", "g": "cq"}
+    count = {"cv": 0, "ca": 0, "cp": 0, "cq": 0, "sent": 0}
+    known = {k: {} for k in Q}
+    wrote, readers = {}, {}
+    ndma = [0]
+
+    def wait(qn, ev):
+        sem, val, clock = ev
+        if qn == "p" and sem == "cp":
+            return
+        kn = known[qn]
+        if kn.get(sem, 0) < val:
+            Q[qn].wait_ge(T.sem[sem], val)
+            kn[sem] = val
+        for s2, v2 in clock.items():
+            if kn.get(s2, 0) < v2:
+                kn[s2] = v2
+
+    def before(qn, R, Wr):
+        evs = []
+        for t in R:
+            evs += wrote.get(t, [])
+            if t[0] == "P":
+                evs += [e for e in readers.get(t, []) if e[0] != CS.get(qn)]
+        for t in Wr:
+            evs += wrote.get(t, []) + readers.get(t, [])
+        best = {}
+        for e in evs:
+            if e[0] not in best or best[e[0]][1] < e[1]:
+                best[e[0]] = e
+        for e in best.values():
+            wait(qn, e)
+
+    def after(ev, R, Wr):
+        for t in R:
+            readers.setdefault(t, []).append(ev)
+        for t in Wr:
+            wrote[t] = [ev]
+            readers[t] = []
+
+    def op(qn, R, Wr, fn):
+        R, Wr = R.split(), Wr.split()
+        before(qn, R, Wr)
+        ins = fn(Q[qn])
+        sem = CS[qn]
+        for i in (ins if isinstance(ins, list) else [ins]):
+            i.then_inc(T.sem[sem], 1)
+            count[sem] += 1
+        after((sem, count[sem], dict(known[qn])), R, Wr)
+
+    def dma(qn, R, Wr, out, in_):
+        R, Wr = R.split(), Wr.split()
+        before(qn, R, Wr)
+        sem = "d%d" % ndma[0]
+        ndma[0] += 1
+        Q[qn].dma_start(out, in_).then_inc(T.sem[sem], 16)
+        count[sem] = 16
+        after((sem, 16, dict(known[qn])), R, Wr)
+
+    def send(R, trs, n):
+        before("g", R.split(), [])
+        g.remote_dma_fused(trs, local_sem=T.sem.sent)
+        count["sent"] += n
+
+    def arrives(tok, sem, n):
+        count[sem] = n
+        wrote[tok] = [(sem, n, {})]
+
+    def ts(R, Wr, out, in0, s1, o1, s2=None, o2=None):
+        if o2 is None:
+            op("v", R, Wr, lambda e: e.tensor_scalar(out, in0, s1, None, o1))
+        else:
+            op("v", R, Wr, lambda e: e.tensor_scalar(out, in0, s1, s2, o1, o2))
+
+    def tt(R, Wr, out, a, b, o):
+        op("v", R, Wr, lambda e: e.tensor_tensor(out, a, b, o))
+
+    def cp(R, Wr, out, in_):
+        op("v", R, Wr, lambda e: e.tensor_copy(out, in_))
+
+    def ms(Wr, ap, val):
+        op("v", "", Wr, lambda e: e.memset(ap, val))
+
+    def act(R, Wr, out, in_, f=F.Identity, **kw):
+        op("a", R, Wr, lambda e: e.activation(out, in_, f, **kw))
+
+    def mm(R, Wr, items, each):
+        def fn(e):
+            ins = [e.matmul(*it) for it in items]
+            return ins if each else ins[-1]
+        op("p", R, Wr, fn)
+
+    def sel(R, Wr, out, in_, pat, cmp, base, cm):
+        op("g", R, Wr, lambda e: e.affine_select(out, in_, pat, cmp, 0.0, base, cm))
+
+    def iota(Wr, out, pat, base, cm, **kw):
+        op("g", "", Wr, lambda e: e.iota(out, pat, base, cm, **kw))
+
+    def tk(s, k):
+        return s.replace("#", str(k))
+
+    P = [T["P%d" % b] for b in range(8)]
+    off = topo.engines(core, cores[order[me][0]])
+    on = [e for e in topo.engines(core, cores[order[me][4]]) if e not in off]
+    AND, SHR = A.bitwise_and, A.arith_shift_right
+
+    dma("s", "", "tm", T.tm_i[:], T.tm[:])
+    dma("s", "", "sh00", T.shI[0::2, 0:256], T.sh[:, 0:2048])
+    dma("a", "", "sh01", T.shI[1::2, 0:256], T.sh[:, 0:2048])
+    dma("s", "", "pix", T.pix_i[:], T.pix[:])
+    dma("s", "", "pol", T.pol_i[:], T.pol[:])
+    dma("s", "", "last", T.last_i[:], T.last[:])
+    dma("s", "", "sh10", T.shI[0::2, 256:512], T.sh[:, 2048:4096])
+    dma("s", "", "sh11", T.shI[1::2, 256:512], T.sh[:, 2048:4096])
+    dma("s", "", "rate", T.rate_s[:], T.rate[:], )
+    dma("s", "", "V", T.V[:, 0:S], T.v[:])
+
+    iota("k16", T.k16[:], [[-1, 16]], 16, 1)
+    iota("colI", T.colI[:], [[1, 48]], 0, 0)
+    ms("ones", T.ones[:], 1.0)
+    ms("negb", T.negb[:], -1.0)
+    lo, hi, dg = [[-16, 8], [0, 16]], [[16, 8], [0, 16]], [[-1, 128]]
+    sel("ones", "B1", T.B1[:], T.ones[:, 0:128], lo, A.is_ge, 0, 1)
+    sel("B1", "B", T.B[:], T.B1[:], hi, A.is_ge, 15, -1)
+    sel("negb", "U1", T.U1[:], T.negb[:], dg, A.is_gt, 0, 1)
+    sel("U1", "U", T.U[:], T.U1[:], hi, A.is_ge, 15, -1)
+    sel("ones", "ident", T.ident[:], T.ones[:, 0:128], dg, A.is_equal, 0, 1)
+    small = dict(allow_small_or_imprecise_dtypes=True)
+    for k in range(2):
+        iota(tk("W#", k), T.W[:, cs_(1024 * k, 1024)], [[0, 8], [256, 128]], 256 * (S + CAP * me - OFFC), 0, **small)
+    iota("big", T.big[:], [[0, 2048]], 1, 0, **small)
+    act("ones", "C0", T.C0[:], T.ones[:, 0:128], F.Exp, scale=-200.0)
+    ts("k16", "k15", T.k15[:], T.k16[:], 15, AND)
+    ts("k16", "parI", T.parI[:], T.k16[:, 0:1], 1, AND)
+    ts("k15", "t16", T.t16[:], T.k15[:], 0.0, A.is_equal)
+    cp("k15", "pcol", T.pcol[:], T.k15[:, 0:1])
+    cp("parI", "par", T.par[:], T.parI[:])
+    tt("t16", "tbl", T.tbl[:], T.t16[:, 0::2], T.t16[:, 1::2], A.add)
+    ts("colI pcol", "pmU", T.pmU[:], T.colI[:], 0.0, A.mult, T.pcol[:], A.add)
+    cp("colI", "colU", T.colU[:], T.colI[:])
+    act("t16 pmU", "dmask", T.dmask[:], T.t16[:].indirect(T.pmU[:]))
+    ms("reset", T.reset[:], 1.0)
+    ms("Zb", T.Zb[:], 0.0)
+    ms("Zf", T.Zf[:], 0.0)
+    ms("C1", T.C1[:], 16.0)
+    ms("negf", T.negf[:], -1.0)
+    ms("onef", T.onef[:], 1.0)
+    ms("reset", T.reset[:, 0::48], 0.0)
+    cp("B", "Zb", T.Zb[:, 15:128:16], T.B[:, 0::16])
+    cp("B", "Zf", T.Zf[:, 15:128:16], T.B[:, 0::16])
+
+    ts("tm", "hiI", T.hiI[:], T.tm_i[:], 8, SHR)
+    ts("tm", "loI", T.loI[:], T.tm_i[:], 255, AND)
+    cp("hiI", "hiU", T.hiU[:], T.hiI[:])
+    cp("loI", "loU", T.loU[:], T.loI[:])
+
+    def split(k):
+        w = cs_(256 * k, 256)
+        ts(tk("sh#0 sh#1 par", k), tk("hs#", k), T.hs[:, w], T.shI[:, w], T.par[:], A.mult)
+        tt(tk("sh#0 sh#1 hs#", k), tk("win#", k), T.win[:, w], T.shI[:, w], T.hs[:, w], A.subtract)
+
+    def shifts(k):
+        for h in (2 * k, 2 * k + 1):
+            w = cs_(384 * h, 384)
+            tt(tk("win# loU mask%d" % h, k), "cand%d" % h, T.cand[:, w],
+               T.win[:, cs_(256 * k, 256)].indirect(T.loU[:, cs_(24 * h, 24)]), T.mask[:, w], A.mult)
+        mm("Zb cand%d cand%d" % (2 * k, 2 * k + 1), "P0",
+           [(P[0][:, 0:48], T.Zb[:, cs_(15 - r, 128)], T.cand[:, 768 * k + r:768 * k + 768:16], r == 0, r == 15)
+            for r in range(16)], False)
+
+    def sort(k, fill):
+        w, wi = cs_(48 * k, 48), cs_(384 * k, 384)
+        tt("P0 pix", tk("u#", k), T.u[:, w], P[0][:, 0:48], T.pix_i[:, w], A.add)
+        ts(tk("u#", k), tk("c#", k), T.c[:, w], T.u[:, w], S - 1, AND)
+        ts(tk("u#", k), tk("q#", k), T.q[:, w], T.u[:, w], 12, SHR, 7, AND)
+        ts(tk("c#", k), tk("c4#", k), T.c4[:, w], T.c[:, w], 4096.0, A.mult)
+        op("v", tk("q#", k), tk("ia#", k),
+           lambda e: e.tensor_scalar(T.ind[:, cs_(384 * k, 48)], T.q[:, w], 0.0, None, A.is_equal))
+        tt(tk("c4# tp", k), tk("pay#", k), T.pay[:, w], T.c4[:, w], T.tp[:, w], A.add)
+        act(tk("pay# colU", k), tk("gexp#", k), T.gexp[:, cs_(768 * k, 768)], T.pay[:, w].indirect(T.colU[:]))
+        op("v", tk("q#", k), tk("ind#", k),
+           lambda e: [e.tensor_scalar(T.ind[:, cs_(384 * k + 48 * j, 48)], T.q[:, w], float(j), None, A.is_equal)
+                      for j in range(1, 8)])
+        op("v", tk("reset ia# ind#", k), tk("scn#", k),
+           lambda e: e.tensor_tensor_scan(T.scn[:, wi], T.reset[:], T.ind[:, wi], 0.0, A.mult, A.add))
+        mm(tk("U ia# ind#", k), "P1", [(P[1][:, 0:384], T.U[:], T.ind[:, wi], True, False)], True)
+        mm(tk("B scn#", k), "P1", [(P[1][:, 0:384], T.B[:], T.scn[:, wi], False, True)], True)
+        ts(tk("q#", k), tk("qb#", k), T.qb[:, w], T.q[:, w], 128.0, A.mult)
+        tt(tk("P1 ia# ind#", k), tk("M#", k), T.M[:, wi], T.ind[:, wi], P[1][:, 0:384], A.mult)
+        mm(tk("ident qb#", k), "P2", [(P[2][:, 0:48], T.ident[:], T.qb[:, w], True, False)], True)
+        mm(tk("ident M#", k), "P2", [(P[2][:, 0:48], T.ident[:], T.M[:, cs_(384 * k + 48 * j, 48)], False, j == 7)
+                                     for j in range(8)], False)
+        fill()
+        ts("P2", tk("slot#", k), T.slot[:, w], P[2][:, 0:48], -1.0, A.add)
+        tt(tk("gexp# dmask slot#", k), tk("W#", k), T.W[:, cs_(1024 * k, 1024)].indirect(T.slot[:, w]),
+           T.gexp[:, cs_(768 * k, 768)], T.dmask[:], A.mult)
+        mm(tk("Zf W#", k), "P3",
+           [(P[3][:, 0:64], T.Zf[:, cs_(15 - r, 128)], T.W[:, 1024 * k + r:1024 * k + 1024:16], r == 0, r == 15)
+            for r in range(16)], False)
+
+    def paysend(k, f):
+        f("P3", tk("psend#", k), T.psend[:, cs_(64 * k, 64)], P[3][:, 0:64])
+        f("P3", tk("pown#", k), T.pland[:, cs_(64 * k + 56, 8)], P[3][:, cs_(8 * me, 8)])
+        trs, n = [], 0
+        near = [on[0:2], on[2:4], on[4:6]] if k == 0 else [on[4:8], on[0:2], on[2:4]]
+        for j, o in enumerate(order[me][:7]):
+            es = off[2 * j:2 * j + 2] if j < 4 else near[j - 4]
+            trs.append(transfer(topo, cores[o], es, T.sem[tk("pay#", k)], T.psend[:, cs_(64 * k + 8 * o, 8)],
+                                T.pland[:, cs_(64 * k + 8 * order[o].index(me), 8)]))
+            n += len(es)
+        send(tk("psend#", k), trs, n)
+        arrives(tk("pland#", k), tk("pay#", k), n)
+
+    def dtinit(k):
+        for b in (6 - 2 * k, 7 - 2 * k):
+            mm(tk("ones C#", k), "P%d" % b, [(P[b][:], T[tk("C#", k)][:], T.ones[:], True, False)], True)
+
+    split(0)
+    for h in range(4):
+        act("tbl hiU", "mask%d" % h, T.mask[:, cs_(384 * h, 384)], T.tbl[:].indirect(T.hiU[:, cs_(24 * h, 24)]))
+    shifts(0)
+    ts("pol", "ta", T.ta[:], T.pol_i[:], 0.5, A.mult, 0.5, A.add)
+    ts("tm", "tb", T.tb[:], T.tm_i[:], 2.0, A.mult, -4096.0 * OFFC, A.add)
+    tt("ta tb", "tp", T.tp[:], T.ta[:], T.tb[:], A.add)
+    sort(0, lambda: cp("last", "lf", T.lf[:], T.last_i[:]))
+    op("a", "lf t16", "L", lambda e: [e.activation(T.L[:, cs_(256 * h, 256)], T.lf[:], F.Identity,
+                                                   scale=T.t16[:, h:h + 1]) for h in range(16)])
+    split(1)
+    shifts(1)
+    paysend(0, cp)
+    sel("big", "Rep", T.Rep[:], T.big[:], [[-1, 16], [-16, 8], [0, 16]], A.is_equal, 0, 1)
+    sel("negf", "nB1", T.nB1[:], T.negf[:], lo, A.is_ge, 0, 1)
+    sel("nB1", "nB", T.nB[:], T.nB1[:], hi, A.is_ge, 15, -1)
+    sel("onef", "idf", T.idf[:], T.onef[:], dg, A.is_equal, 0, 1)
+    ts("rate", "nrate", T.nrate[:], T.rate_s[:], -1.0, A.mult)
+
+    def fill1():
+        dtinit(0)
+        dtinit(1)
+    sort(1, fill1)
+
+    def lists_a(k):
+        w = cs_(64 * k, 64)
+        cp(tk("pland# pown#", k), tk("xi#", k), T.xi[:, w], T.pland[:, w])
+        ts(tk("xi#", k), tk("ci#", k), T.ci[:, w], T.xi[:, w], 12, SHR)
+        ts(tk("xi#", k), tk("ti#", k), T.ti[:, w], T.xi[:, w], 1, SHR, 2047, AND)
+        ts(tk("ci#", k), tk("cg#", k), T.cg[:, w], T.ci[:, w], float(OFFC), A.add, float(S - 1), A.min)
+        cp(tk("ti#", k), tk("th#", k), T.th[:, w], T.ti[:, w])
+        for h in range(2):
+            act(tk("L cg#", k), tk("Lg#%d" % h, k), T.Lg[:, cs_(1024 * k + 512 * h, 512)],
+                T.L[:, 0:S].indirect(T.cg[:, cs_(64 * k + 32 * h, 32)]))
+
+    def lists_b(k):
+        w = cs_(64 * k, 64)
+        ts(tk("xi#", k), tk("pi#", k), T.pi[:, w], T.xi[:, w], 1, AND)
+        ts(tk("ci#", k), tk("cs#", k), T.cs[:, w], T.ci[:, w], float(OFFC), A.add)
+        ts(tk("cg#", k), tk("n1#", k), T.n1[:, w], T.cg[:, w], -1.0, A.add, 0.0, A.max)
+        ts(tk("pi#", k), tk("wb#", k), T.wb[:, w], T.pi[:, w], 2.0, A.mult, -1.0, A.add)
+        ts(tk("ci#", k), tk("n2#", k), T.n2[:, w], T.ci[:, w], OFFC + 1.0, A.add, float(S - 1), A.min)
+        ts(tk("cg#", k), tk("n3#", k), T.n3[:, w], T.cg[:, w], -256.0, A.add, 0.0, A.max)
+        ts(tk("ci#", k), tk("n4#", k), T.n4[:, w], T.ci[:, w], OFFC + 256.0, A.add, float(S - 1), A.min)
+
+    def reps(b, name, k, h, closed):
+        mm(tk("Rep %s#" % name, k), "P%d" % b,
+           [(P[b][:, r::16], T.Rep[:, cs_(128 * r, 128)], T[name][:, cs_(64 * k + 32 * h, 32)], closed, closed)
+            for r in range(16)], True)
+
+    def decay(k):
+        for h in range(2):
+            b, w = 6 - 2 * k + h, cs_(1024 * k + 512 * h, 512)
+            reps(b, "th", k, h, False)
+            mm(tk("nB Lg#%d" % h, k), "P%d" % b, [(P[b][:], T.nB[:], T.Lg[:, w], False, True)], True)
+            act("P%d nrate" % b, tk("Ex#%d" % h, k), T.Ex[:, w], P[b][:], F.Exp, scale=T.nrate[:])
+
+    def signs(k, part):
+        for h in range(2):
+            b = 6 * k + h
+            if part == "p":
+                reps(b, "wb", k, h, True)
+            else:
+                act("P%d" % b, tk("wr#%d" % h, k), T.wr[:, cs_(1024 * k + 512 * h, 512)], P[b][:])
+
+    def product(k):
+        w = cs_(1024 * k, 1024)
+        tt(tk("V cg# Ex#0 Ex#1", k), tk("prod#", k), T.prod[:, w], T.V[:, 0:S].indirect(T.cg[:, cs_(64 * k, 64)]),
+           T.Ex[:, w], A.mult)
+
+    def update(k):
+        w = cs_(1024 * k, 1024)
+        tt(tk("prod# wr#0 wr#1 cs#", k), "V", T.V[:].indirect(T.cs[:, cs_(64 * k, 64)]), T.prod[:, w], T.wr[:, w],
+           A.add)
+
+    def answers(k, fill, fill2):
+        mine = T.ans[:, cs_(1024 * k + 128 * me, 128)]
+        steps = []
+        for b0, b1, how in CHUNKS[k]:
+            w = slice(1024 * k + 128 * b0, 1024 * k + 128 * b1)
+            t = {n: " ".join("%s%d_%d" % (n, k, j) for j in range(b0, b1)) for n in ("N1", "N3", "N4", "acc", "OUT")}
+            nb = {n: T.V[:, 0:S].indirect(T[n][:, 64 * k + 8 * b0:64 * k + 8 * b1]) for n in ("n1", "n2", "n3", "n4")}
+            out = mine if b1 == 8 else T.OUT[:, w]
+            if how == "p":
+                ps = P[0][:, 0:128 * (b1 - b0)]
+                for j, (buf, n) in enumerate([("N1", "n1"), ("N3", "n3"), ("acc", "n2"), ("N4", "n4")]):
+                    act(tk("V %s#" % n, k), t[buf], T[buf][:, w], nb[n])
+                    mm("idf " + t[buf], "P0", [(ps, T.idf[:], T[buf][:, w], j == 0, j == 3)], True)
+                fill2()
+                act("P0", t["OUT"], out, ps)
+                continue
+            act(tk("V n1#", k), t["N1"], T.N1[:, w], nb["n1"])
+            steps.append([(tk("V n2# ", k) + t["N1"], t["acc"], T.acc[:, w], nb["n2"], T.N1[:, w]),
+                          (tk("V n3# ", k) + t["acc"], t["N3"], T.N3[:, w], nb["n3"], T.acc[:, w]),
+                          (tk("V n4# ", k) + t["N3"], t["OUT"], out, nb["n4"], T.N3[:, w])])
+        fill()
+        seq = steps[0][:-1]
+        for i in range(len(steps)):
+            nxt = steps[i + 1] if i + 1 < len(steps) else []
+            seq += nxt[:1] + steps[i][-1:] + nxt[1:-1]
+        for s in seq:
+            tt(s[0], s[1], s[2], s[3], s[4], A.add)
+
+        def go(ps, ess):
+            trs = []
+            for p, es in zip(ps, ess):
+                src = T.OUT[:, cs_(1024 * k + 128 * p, 128)]
+                if p < 2:
+                    trs.append(transfer(topo, helper[me][p], es, T.sem[tk("rel#", k)], src, T.rel[:, cs_(128 * k, 128)]))
+                else:
+                    trs.append(transfer(topo, cores[order[me][p]], es, T.sem[tk("ans#", k)], src, mine))
+            send(" ".join("OUT%d_%d" % (k, p) for p in ps), trs, 8)
+        for p in range(2):
+            go([p], [on if topo.chip(helper[me][p]) == topo.chip(core) else off])
+        go([2, 3], [off[0:4], off[4:8]])
+        for ps in ([[4, 5], [6]] if k == 0 else [[6], [4, 5]]):
+            go(ps, [on] if len(ps) == 1 else [on[0:4], on[4:8]])
+        arrives(tk("ans#", k), tk("ans#", k), 40)
+
+    def back(k, f, e0, e1, dq):
+        w, tok = slice(768 * k + e0, 768 * k + e1), "Y%d_%d" % (k, e0)
+        f(tk("ans# OUT#_7 slot#", k), tok, T.Y[:, w],
+          T.ans[:, cs_(1024 * k, 1024)].indirect(T.slot[:, 48 * k + e0 // 16:48 * k + e1 // 16]))
+        if k == 0:
+            wait(dq, ("sent", count["sent"], {}))
+        dma(dq, tok, "", T.y[:, w], T.Y[:, w])
+
+    lists_a(0)
+    op("v", "ti0 t16", "A0", lambda e: [e.tensor_scalar(T.A0[:, r::16], T.ti[:, 0:64], T.t16[:, r:r + 1], None, A.mult)
+                                        for r in range(16)])
+    lists_b(0)
+    cp("A0 cs0", "L", T.L[:].indirect(T.cs[:, 0:64]), T.A0[:])
+    paysend(1, act)
+    decay(0)
+    signs(0, "p")
+    signs(0, "a")
+    product(0)
+    lists_a(1)
+    update(0)
+    decay(1)
+    lists_b(1)
+    signs(1, "p")
+    answers(0, lambda: product(1), lambda: signs(1, "a"))
+    update(1)
+    answers(1, lambda: None, lambda: None)
+    back(0, cp, 0, 768, "s")
+    back(1, cp, 0, 384, "s")
+    back(1, act, 384, 768, "a")
+    for sem, n in count.items():
+        g.wait_ge(T.sem[sem], n)

@@ -3,28 +3,27 @@ from concourse.mybir import AluOpType as A, ActivationFunctionType as F
 
 NC = 64
 E, CAP, S = 768, 128, 4096
-OFFC = 2560
+WIN = 5248
 
 I32, F32, BF, U16, F16 = "int32", "float32", "bfloat16", "uint16", "float16"
 _SB = {
-    I32: dict(tm_i=96, pix_i=96, pol_i=96, shI=512, last_i=256, k16=16, k15=16, parI=1, colI=48, hiI=96, loI=96,
-              u=96, q=96, c=96, xi=128, ci=128, ti=128, pi=128),
-    F32: dict(rate_s=1, V=5120, L=5120, W=2048, t16=16, tbl=8, pcol=1, par=1, dmask=768, negf=128, onef=128, nB1=128,
-              nB=128, idf=128, Zf=144, nrate=1, lf=256, win=512, mask=1536, ta=96, tb=96, tp=96, c4=96, pay=96,
-              gexp=1536, psend=128, pland=128, Lg=2048, Ex=2048, wr=2048, prod=2048, A0=1024, N1=2048, N3=2048,
-              N4=2048, acc=2048, OUT=2048, ans=2048, Y=1536, rel=256),
-    BF: dict(ones=512, big=2048, negb=128, B1=128, B=128, U1=128, U=128, ident=128, Zb=144, Rep=2048, reset=384,
-             C0=128, C1=128, hs=512, cand=1536, qb=96, ind=768, scn=768, M=768, wb=128),
-    U16: dict(colU=48, pmU=48, hiU=96, loU=96, slot=96, cg=128, cs=128, n1=128, n2=128, n3=128, n4=128),
-    F16: dict(th=128)}
+    I32: dict(tm_i=96, pix_i=96, pol_i=96, shI=512, last_i=256, k3=40, k15=40, parI=1, p4I=1, colI=48, hiI=96, loI=96,
+              u=96, q=96, cc=192, xi=128, ci=128, ti=128, pi=128),
+    F32: dict(rate_s=1, V=WIN, L=WIN, t16=16, tbl=8, t4=16, pcol=1, par=1, p4=1, w1=1, wcol=1, spare=64, spw=64,
+              idf=128, nrate=1, e1=1, lf=256, win=256, candf=768, Zf=144, mask=1536, psend=128, pland=128, Ex=2048, wr=2048,
+              prod=2048, dts=1024, N1=2048, N3=2048, N4=2048, acc=2048, OUT=2048, ans=2048, Y=1536, rel=256),
+    BF: dict(ones=528, B1=128, B=128, U=128, ident=128, Zb=144, Rep=2048, reset=384, Q=528, J=384, nB=128, C0=128,
+             C1=128, C2=128, hs=256, cand=768, ind=768, scn=768, wb=128, cb=192, tb=288, X=384, dmask=384,
+             gexp=1536, W=2048),
+    U16: dict(xU=48, pmU=48, hiU=96, loU=96, slot=96, cg=128, cs=128, n1=128, n2=128, n3=128, n4=128),
+    F16: dict(th=128, M=768, Lg=2048)}
 SCRATCH = {n: ("sbuf", [128, w], d) for d, ws in _SB.items() for n, w in ws.items()}
 for _b in range(8):
     SCRATCH["P%d" % _b] = ("psum", [128, 512], F32)
 SEMAPHORES = ["cv", "ca", "cp", "cq", "sent", "pay0", "pay1", "ans0", "ans1", "rel0", "rel1"] + \
              ["d%d" % i for i in range(16)]
 
-CHUNKS = [[(0, 2, "v"), (2, 4, "v"), (7, 8, "v"), (4, 7, "p")],
-          [(0, 1, "v"), (1, 2, "v"), (2, 4, "v"), (6, 7, "v"), (7, 8, "v"), (4, 6, "p")]]
+CHUNKS = [(0, 1, "v"), (1, 2, "v"), (2, 4, "v"), (6, 7, "v"), (7, 8, "v"), (4, 6, "p")]
 
 
 def cs_(a, n):
@@ -182,104 +181,133 @@ def rank_program(g, core, T, topo):
     off = topo.engines(core, cores[order[me][0]])
     on = [e for e in topo.engines(core, cores[order[me][4]]) if e not in off]
     AND, SHR = A.bitwise_and, A.arith_shift_right
+    EMPTY = 2 ** 21
 
     dma("s", "", "tm", T.tm_i[:], T.tm[:])
-    dma("s", "", "sh00", T.shI[0::2, 0:256], T.sh[:, 0:2048])
     dma("a", "", "sh01", T.shI[1::2, 0:256], T.sh[:, 0:2048])
+    dma("s", "", "sh00", T.shI[0::2, 0:256], T.sh[:, 0:2048])
     dma("s", "", "pix", T.pix_i[:], T.pix[:])
     dma("s", "", "pol", T.pol_i[:], T.pol[:])
-    dma("s", "", "last", T.last_i[:], T.last[:])
     dma("s", "", "sh10", T.shI[0::2, 256:512], T.sh[:, 2048:4096])
     dma("s", "", "sh11", T.shI[1::2, 256:512], T.sh[:, 2048:4096])
-    dma("s", "", "rate", T.rate_s[:], T.rate[:], )
+    dma("s", "", "last", T.last_i[:], T.last[:])
+    dma("s", "", "rate", T.rate_s[:], T.rate[:])
     dma("s", "", "V", T.V[:, 0:S], T.v[:])
 
-    iota("k16", T.k16[:], [[-1, 16]], 16, 1)
+    small = dict(allow_small_or_imprecise_dtypes=True)
+    iota("ka", T.k3[:, 0:16], [[-1, 16]], 16, 1)
+    iota("kb", T.k3[:, 16:24], [[-2, 8]], 16, 1)
+    iota("kc", T.k3[:, 24:40], [[-4, 4], [0, 4]], 16, 1)
     iota("colI", T.colI[:], [[1, 48]], 0, 0)
     ms("ones", T.ones[:], 1.0)
-    ms("negb", T.negb[:], -1.0)
     lo, hi, dg = [[-16, 8], [0, 16]], [[16, 8], [0, 16]], [[-1, 128]]
     sel("ones", "B1", T.B1[:], T.ones[:, 0:128], lo, A.is_ge, 0, 1)
     sel("B1", "B", T.B[:], T.B1[:], hi, A.is_ge, 15, -1)
-    sel("negb", "U1", T.U1[:], T.negb[:], dg, A.is_gt, 0, 1)
-    sel("U1", "U", T.U[:], T.U1[:], hi, A.is_ge, 15, -1)
-    sel("ones", "ident", T.ident[:], T.ones[:, 0:128], dg, A.is_equal, 0, 1)
-    small = dict(allow_small_or_imprecise_dtypes=True)
-    for k in range(2):
-        iota(tk("W#", k), T.W[:, cs_(1024 * k, 1024)], [[0, 8], [256, 128]], 256 * (S + CAP * me - OFFC), 0, **small)
-    iota("big", T.big[:], [[0, 2048]], 1, 0, **small)
     act("ones", "C0", T.C0[:], T.ones[:, 0:128], F.Exp, scale=-200.0)
-    ts("k16", "k15", T.k15[:], T.k16[:], 15, AND)
-    ts("k16", "parI", T.parI[:], T.k16[:, 0:1], 1, AND)
-    ts("k15", "t16", T.t16[:], T.k15[:], 0.0, A.is_equal)
+    act("B", "nB", T.nB[:], T.B[:], scale=-1.0)
+    sel("ones", "ident", T.ident[:], T.ones[:, 0:128], dg, A.is_equal, 0, 1)
+    sel("ones", "Q", T.Q[:], T.ones[:], [[-1, 4], [-4, 33], [256, 4]], A.is_equal, -768, 1)
+    iota("J", T.J[:], [[128, 8], [0, 48]], 0, 0, **small)
+    sel("nB", "U", T.U[:], T.nB[:], dg, A.is_gt, 0, 1)
+    sel("ones", "reset", T.reset[:], T.ones[:, 0:384], [[0, 8], [1, 48]], A.is_gt, 0, 0)
+    iota("W1", T.W[:, 1024:2048], [[0, 1024]], EMPTY, 0, **small)
+
+    def repeat(j):
+        sel("ones", "Rep%d" % j, T.Rep[:, cs_(512 * j, 512)], T.ones[:, 0:512], [[-1, 4], [-16, 8], [0, 16]],
+            A.is_equal, -4 * j, 1)
+    repeat(0)
+    repeat(1)
+    ms("W0", T.W[:, 0:1024], float(EMPTY))
+    ts("ka kb kc", "k15", T.k15[:], T.k3[:], 15, AND)
+    ts("ka", "parI", T.parI[:], T.k3[:, 0:1], 1, AND)
+    ts("ka", "p4I", T.p4I[:], T.k3[:, 0:1], 3, AND)
     cp("k15", "pcol", T.pcol[:], T.k15[:, 0:1])
-    cp("parI", "par", T.par[:], T.parI[:])
-    tt("t16", "tbl", T.tbl[:], T.t16[:, 0::2], T.t16[:, 1::2], A.add)
+    ts("k15", "t4", T.t4[:], T.k15[:, 24:40], 4.0, A.is_lt)
+    ts("k15", "tbl", T.tbl[:], T.k15[:, 16:24], 2.0, A.is_lt)
     ts("colI pcol", "pmU", T.pmU[:], T.colI[:], 0.0, A.mult, T.pcol[:], A.add)
-    cp("colI", "colU", T.colU[:], T.colI[:])
-    act("t16 pmU", "dmask", T.dmask[:], T.t16[:].indirect(T.pmU[:]))
-    ms("reset", T.reset[:], 1.0)
+    act("t4 pmU", "dmask", T.dmask[:], T.t4[:].indirect(T.pmU[:, 0:24]))
+    cp("parI", "par", T.par[:], T.parI[:])
+    ts("k15", "t16", T.t16[:], T.k15[:, 0:16], 1.0, A.is_lt)
+    ts("p4I", "p4", T.p4[:], T.p4I[:], 48.0, A.mult)
+    ts("p4I", "w1", T.w1[:], T.p4I[:], 2.0, A.is_lt, 4095.0, A.mult)
     ms("Zb", T.Zb[:], 0.0)
-    ms("Zf", T.Zf[:], 0.0)
-    ms("C1", T.C1[:], 16.0)
-    ms("negf", T.negf[:], -1.0)
-    ms("onef", T.onef[:], 1.0)
-    ms("reset", T.reset[:, 0::48], 0.0)
+    ts("colI p4", "xU", T.xU[:], T.colI[:], T.p4[:], A.add)
+    ts("w1", "wcol", T.wcol[:], T.w1[:], 1.0, A.add)
     cp("B", "Zb", T.Zb[:, 15:128:16], T.B[:, 0::16])
-    cp("B", "Zf", T.Zf[:, 15:128:16], T.B[:, 0::16])
+    act("Zb", "Zf", T.Zf[:], T.Zb[:], scale=0.5)
 
     ts("tm", "hiI", T.hiI[:], T.tm_i[:], 8, SHR)
     ts("tm", "loI", T.loI[:], T.tm_i[:], 255, AND)
     cp("hiI", "hiU", T.hiU[:], T.hiI[:])
+    ts("sh00 sh01 par", "hs", T.hs[:], T.shI[:, 0:256], T.par[:], A.mult)
     cp("loI", "loU", T.loU[:], T.loI[:])
+    tt("sh00 sh01 hs", "win", T.win[:], T.shI[:, 0:256], T.hs[:], A.subtract)
 
-    def split(k):
-        w = cs_(256 * k, 256)
-        ts(tk("sh#0 sh#1 par", k), tk("hs#", k), T.hs[:, w], T.shI[:, w], T.par[:], A.mult)
-        tt(tk("sh#0 sh#1 hs#", k), tk("win#", k), T.win[:, w], T.shI[:, w], T.hs[:, w], A.subtract)
+    def cand(h):
+        w, R = cs_(384 * (h % 2), 384), " loU mask%d" % h
+        out, window = (T.cand, T.win[:]) if h < 2 else (T.candf, T.shI[:, 256:512])
+        tt(("win" if h < 2 else "sh10 sh11") + R, "cand%d" % h, out[:, w],
+           window.indirect(T.loU[:, cs_(24 * h, 24)]), T.mask[:, cs_(384 * h, 384)], A.mult)
 
     def shifts(k):
-        for h in (2 * k, 2 * k + 1):
-            w = cs_(384 * h, 384)
-            tt(tk("win# loU mask%d" % h, k), "cand%d" % h, T.cand[:, w],
-               T.win[:, cs_(256 * k, 256)].indirect(T.loU[:, cs_(24 * h, 24)]), T.mask[:, w], A.mult)
-        mm("Zb cand%d cand%d" % (2 * k, 2 * k + 1), "P0",
-           [(P[0][:, 0:48], T.Zb[:, cs_(15 - r, 128)], T.cand[:, 768 * k + r:768 * k + 768:16], r == 0, r == 15)
-            for r in range(16)], False)
+        Z, c = (T.Zf, T.candf) if k else (T.Zb, T.cand)
+        mm("Zb Zf cand%d cand%d" % (2 * k, 2 * k + 1), "P0",
+           [(P[0][:, 0:48], Z[:, cs_(15 - r, 128)], c[:, r:768:16], r == 0, r == 15) for r in range(16)], False)
 
-    def sort(k, fill):
+    def quads(k, R, pieces, last):
+        items = [(P[4 + k][:, cs_(48 * v, 48)], T.Q[:, cs_(132 * v + 3 - b, 128)], src, False, False)
+                 for v in range(4) for b, src in pieces]
+        items[-1] = items[-1][:4] + (last,)
+        mm("Q " + R, "P%d" % (4 + k), items, False)
+
+    def early(k):
+        mm("ones C0", "P%d" % (4 + k), [(P[4 + k][:, 0:192], T.C0[:], T.ones[:, 0:192], True, False)], True)
+        quads(k, "tb0 tb1 tb2", [(2, T.tb[:, cs_(48 * k, 48)]), (2, T.tb[:, cs_(96 + 48 * k, 48)]),
+                                 (3, T.tb[:, cs_(192 + 48 * k, 48)])], False)
+
+    def base():
+        mm("ident J", "P1", [(P[1][:, 0:384], T.ident[:], T.J[:], True, False)], True)
+
+    def sort(k, fill0, fill1, fill2):
         w, wi = cs_(48 * k, 48), cs_(384 * k, 384)
         tt("P0 pix", tk("u#", k), T.u[:, w], P[0][:, 0:48], T.pix_i[:, w], A.add)
-        ts(tk("u#", k), tk("c#", k), T.c[:, w], T.u[:, w], S - 1, AND)
+        ts(tk("u#", k), tk("ca#", k), T.cc[:, cs_(96 * k, 48)], T.u[:, w], 0xFC0, AND)
+        ts(tk("u#", k), tk("cc#", k), T.cc[:, cs_(96 * k + 48, 48)], T.u[:, w], 0x3F, AND)
         ts(tk("u#", k), tk("q#", k), T.q[:, w], T.u[:, w], 12, SHR, 7, AND)
-        ts(tk("c#", k), tk("c4#", k), T.c4[:, w], T.c[:, w], 4096.0, A.mult)
-        op("v", tk("q#", k), tk("ia#", k),
-           lambda e: e.tensor_scalar(T.ind[:, cs_(384 * k, 48)], T.q[:, w], 0.0, None, A.is_equal))
-        tt(tk("c4# tp", k), tk("pay#", k), T.pay[:, w], T.c4[:, w], T.tp[:, w], A.add)
-        act(tk("pay# colU", k), tk("gexp#", k), T.gexp[:, cs_(768 * k, 768)], T.pay[:, w].indirect(T.colU[:]))
+        cp(tk("ca# cc#", k), tk("cb#", k), T.cb[:, cs_(96 * k, 96)], T.cc[:, cs_(96 * k, 96)])
+        fill0()
+        quads(k, tk("cb#", k), [(0, T.cb[:, cs_(96 * k, 48)]), (1, T.cb[:, cs_(96 * k + 48, 48)])], True)
+        act("P%d wcol" % (4 + k), tk("X#", k), T.X[:, cs_(192 * k, 192)], P[4 + k][:, 0:192], scale=T.wcol[:])
+        for h in range(2):
+            act(tk("X# xU", k), "gexp%d" % (2 * k + h), T.gexp[:, cs_(768 * k + 384 * h, 384)],
+                T.X[:, cs_(192 * k, 192)].indirect(T.xU[:, cs_(24 * h, 24)]))
         op("v", tk("q#", k), tk("ind#", k),
            lambda e: [e.tensor_scalar(T.ind[:, cs_(384 * k + 48 * j, 48)], T.q[:, w], float(j), None, A.is_equal)
-                      for j in range(1, 8)])
-        op("v", tk("reset ia# ind#", k), tk("scn#", k),
+                      for j in range(8)])
+        op("v", tk("reset ind#", k), tk("scn#", k),
            lambda e: e.tensor_tensor_scan(T.scn[:, wi], T.reset[:], T.ind[:, wi], 0.0, A.mult, A.add))
-        mm(tk("U ia# ind#", k), "P1", [(P[1][:, 0:384], T.U[:], T.ind[:, wi], True, False)], True)
+        mm(tk("U ind#", k), "P1", [(P[1][:, 0:384], T.U[:], T.ind[:, wi], False, False)], True)
         mm(tk("B scn#", k), "P1", [(P[1][:, 0:384], T.B[:], T.scn[:, wi], False, True)], True)
-        ts(tk("q#", k), tk("qb#", k), T.qb[:, w], T.q[:, w], 128.0, A.mult)
-        tt(tk("P1 ia# ind#", k), tk("M#", k), T.M[:, wi], T.ind[:, wi], P[1][:, 0:384], A.mult)
-        mm(tk("ident qb#", k), "P2", [(P[2][:, 0:48], T.ident[:], T.qb[:, w], True, False)], True)
-        mm(tk("ident M#", k), "P2", [(P[2][:, 0:48], T.ident[:], T.M[:, cs_(384 * k + 48 * j, 48)], False, j == 7)
+        fill1()
+        tt(tk("P1 ind#", k), tk("M#", k), T.M[:, wi], T.ind[:, wi], P[1][:, 0:384], A.mult)
+        mm(tk("ident M#", k), "P2", [(P[2][:, 0:48], T.ident[:], T.M[:, cs_(384 * k + 48 * j, 48)], j == 0, j == 7)
                                      for j in range(8)], False)
-        fill()
+        fill2()
         ts("P2", tk("slot#", k), T.slot[:, w], P[2][:, 0:48], -1.0, A.add)
-        tt(tk("gexp# dmask slot#", k), tk("W#", k), T.W[:, cs_(1024 * k, 1024)].indirect(T.slot[:, w]),
-           T.gexp[:, cs_(768 * k, 768)], T.dmask[:], A.mult)
-        mm(tk("Zf W#", k), "P3",
-           [(P[3][:, 0:64], T.Zf[:, cs_(15 - r, 128)], T.W[:, 1024 * k + r:1024 * k + 1024:16], r == 0, r == 15)
+
+    def place(k, h):
+        tt("gexp%d" % (2 * k + h) + tk(" dmask slot#", k), tk("W#", k),
+           T.W[:, cs_(1024 * k, 1024)].indirect(T.slot[:, cs_(48 * k + 24 * h, 24)]),
+           T.gexp[:, cs_(768 * k + 384 * h, 384)], T.dmask[:], A.mult)
+
+    def words(k):
+        mm(tk("Zb W#", k), "P3",
+           [(P[3][:, 0:64], T.Zb[:, cs_(15 - r, 128)], T.W[:, 1024 * k + r:1024 * k + 1024:16], r == 0, r == 15)
             for r in range(16)], False)
 
-    def paysend(k, f):
-        f("P3", tk("psend#", k), T.psend[:, cs_(64 * k, 64)], P[3][:, 0:64])
-        f("P3", tk("pown#", k), T.pland[:, cs_(64 * k + 56, 8)], P[3][:, cs_(8 * me, 8)])
+    def paysend(k):
+        cp("P3", tk("psend#", k), T.psend[:, cs_(64 * k, 64)], P[3][:, 0:64])
+        act(tk("psend#", k), tk("pown#", k), T.pland[:, cs_(64 * k + 56, 8)], T.psend[:, cs_(64 * k + 8 * me, 8)])
         trs, n = [], 0
         near = [on[0:2], on[2:4], on[4:6]] if k == 0 else [on[4:8], on[0:2], on[2:4]]
         for j, o in enumerate(order[me][:7]):
@@ -292,104 +320,128 @@ def rank_program(g, core, T, topo):
 
     def dtinit(k):
         for b in (6 - 2 * k, 7 - 2 * k):
-            mm(tk("ones C#", k), "P%d" % b, [(P[b][:], T[tk("C#", k)][:], T.ones[:], True, False)], True)
+            mm(tk("ones C#", k + 1), "P%d" % b, [(P[b][:], T[tk("C#", k + 1)][:], T.ones[:, 0:512], True, False)], True)
 
-    split(0)
+    def lasts(h0, h1):
+        op("a", "lf t16", " ".join("L%d" % h for h in range(h0, h1)),
+           lambda e: [e.activation(T.L[:, cs_(256 * h, 256)], T.lf[:], F.Identity, scale=T.t16[:, h:h + 1])
+                      for h in range(h0, h1)])
+
     for h in range(4):
         act("tbl hiU", "mask%d" % h, T.mask[:, cs_(384 * h, 384)], T.tbl[:].indirect(T.hiU[:, cs_(24 * h, 24)]))
+    cand(0)
+    cand(1)
     shifts(0)
-    ts("pol", "ta", T.ta[:], T.pol_i[:], 0.5, A.mult, 0.5, A.add)
-    ts("tm", "tb", T.tb[:], T.tm_i[:], 2.0, A.mult, -4096.0 * OFFC, A.add)
-    tt("ta tb", "tp", T.tp[:], T.ta[:], T.tb[:], A.add)
-    sort(0, lambda: cp("last", "lf", T.lf[:], T.last_i[:]))
-    op("a", "lf t16", "L", lambda e: [e.activation(T.L[:, cs_(256 * h, 256)], T.lf[:], F.Identity,
-                                                   scale=T.t16[:, h:h + 1]) for h in range(16)])
-    split(1)
+    ts("hiI", "tb0", T.tb[:, 0:96], T.hiI[:], 256.0, A.mult)
+    ts("pol", "tb1", T.tb[:, 96:192], T.pol_i[:], 1024.0, A.mult, 1024.0, A.add)
+    cp("loI", "tb2", T.tb[:, 192:288], T.loI[:])
+    early(0)
+    base()
+    ts("last", "lf", T.lf[:], T.last_i[:], 2048.0, A.add)
+    lasts(0, 2)
+    sort(0, lambda: None, lambda: cand(2), lambda: cand(3))
     shifts(1)
-    paysend(0, cp)
-    sel("big", "Rep", T.Rep[:], T.big[:], [[-1, 16], [-16, 8], [0, 16]], A.is_equal, 0, 1)
-    sel("negf", "nB1", T.nB1[:], T.negf[:], lo, A.is_ge, 0, 1)
-    sel("nB1", "nB", T.nB[:], T.nB1[:], hi, A.is_ge, 15, -1)
-    sel("onef", "idf", T.idf[:], T.onef[:], dg, A.is_equal, 0, 1)
-    ts("rate", "nrate", T.nrate[:], T.rate_s[:], -1.0, A.mult)
+    early(1)
+    base()
+    place(0, 0)
+    place(0, 1)
+    words(0)
+    lasts(2, 11)
+    sort(1, lambda: paysend(0), lambda: None, lambda: None)
+    iota("C1", T.C1[:], [[0, 128]], 16, 0, **small)
+    iota("spare", T.spare[:], [[16, 64]], S, 1, **small)
+    repeat(2)
+    repeat(3)
+    iota("C2", T.C2[:], [[0, 128]], 32, 0, **small)
+    lasts(11, 16)
+    act("spare", "spw", T.spw[:], T.spare[:], scale=4096.0)
+    act("rate", "nrate", T.nrate[:], T.rate_s[:], scale=-1.0)
+    dtinit(0)
+    place(1, 0)
 
-    def fill1():
-        dtinit(0)
-        dtinit(1)
-    sort(1, fill1)
+    LL = " ".join("L%d" % h for h in range(16))
+    RR = "Rep0 Rep1 Rep2 Rep3 "
 
     def lists_a(k):
         w = cs_(64 * k, 64)
-        cp(tk("pland# pown#", k), tk("xi#", k), T.xi[:, w], T.pland[:, w])
+        tt(tk("pland# pown# spw", k), tk("xi#", k), T.xi[:, w], T.pland[:, w], T.spw[:], A.min)
         ts(tk("xi#", k), tk("ci#", k), T.ci[:, w], T.xi[:, w], 12, SHR)
-        ts(tk("xi#", k), tk("ti#", k), T.ti[:, w], T.xi[:, w], 1, SHR, 2047, AND)
-        ts(tk("ci#", k), tk("cg#", k), T.cg[:, w], T.ci[:, w], float(OFFC), A.add, float(S - 1), A.min)
+        ts(tk("xi#", k), tk("ti#", k), T.ti[:, w], T.xi[:, w], 2047, AND)
+        ts(tk("ci#", k), tk("cg#", k), T.cg[:, w], T.ci[:, w], float(S - 1), A.min)
         cp(tk("ti#", k), tk("th#", k), T.th[:, w], T.ti[:, w])
-        for h in range(2):
-            act(tk("L cg#", k), tk("Lg#%d" % h, k), T.Lg[:, cs_(1024 * k + 512 * h, 512)],
-                T.L[:, 0:S].indirect(T.cg[:, cs_(64 * k + 32 * h, 32)]))
 
-    def lists_b(k):
+    def lists_w(k):
         w = cs_(64 * k, 64)
-        ts(tk("xi#", k), tk("pi#", k), T.pi[:, w], T.xi[:, w], 1, AND)
-        ts(tk("ci#", k), tk("cs#", k), T.cs[:, w], T.ci[:, w], float(OFFC), A.add)
-        ts(tk("cg#", k), tk("n1#", k), T.n1[:, w], T.cg[:, w], -1.0, A.add, 0.0, A.max)
-        ts(tk("pi#", k), tk("wb#", k), T.wb[:, w], T.pi[:, w], 2.0, A.mult, -1.0, A.add)
-        ts(tk("ci#", k), tk("n2#", k), T.n2[:, w], T.ci[:, w], OFFC + 1.0, A.add, float(S - 1), A.min)
-        ts(tk("cg#", k), tk("n3#", k), T.n3[:, w], T.cg[:, w], -256.0, A.add, 0.0, A.max)
-        ts(tk("ci#", k), tk("n4#", k), T.n4[:, w], T.ci[:, w], OFFC + 256.0, A.add, float(S - 1), A.min)
+        ts(tk("xi#", k), tk("pi#", k), T.pi[:, w], T.xi[:, w], 2048, AND)
+        cp(tk("ci#", k), tk("cs#", k), T.cs[:, w], T.ci[:, w])
+        ts(tk("pi#", k), tk("wb#", k), T.wb[:, w], T.pi[:, w], 1.0 / 1024, A.mult, -1.0, A.add)
+
+    def lists_n():
+        ts("cg0 cg1", "n10 n11", T.n1[:], T.cg[:], -1.0, A.add, 0.0, A.max)
+        ts("cg0 cg1", "n20 n21", T.n2[:], T.cg[:], 1.0, A.add, float(S - 1), A.min)
+        ts("cg0 cg1", "n30 n31", T.n3[:], T.cg[:], -256.0, A.add, 0.0, A.max)
+        ts("cg0 cg1", "n40 n41", T.n4[:], T.cg[:], 256.0, A.add, float(S - 1), A.min)
+
+    def lgather(k, h):
+        act(LL + tk(" cg#", k), tk("Lg#%d" % h, k), T.Lg[:, cs_(1024 * k + 512 * h, 512)],
+            T.L[:, 0:S].indirect(T.cg[:, cs_(64 * k + 32 * h, 32)]))
 
     def reps(b, name, k, h, closed):
-        mm(tk("Rep %s#" % name, k), "P%d" % b,
+        mm(RR + tk("%s#" % name, k), "P%d" % b,
            [(P[b][:, r::16], T.Rep[:, cs_(128 * r, 128)], T[name][:, cs_(64 * k + 32 * h, 32)], closed, closed)
             for r in range(16)], True)
 
-    def decay(k):
-        for h in range(2):
-            b, w = 6 - 2 * k + h, cs_(1024 * k + 512 * h, 512)
-            reps(b, "th", k, h, False)
-            mm(tk("nB Lg#%d" % h, k), "P%d" % b, [(P[b][:], T.nB[:], T.Lg[:, w], False, True)], True)
-            act("P%d nrate" % b, tk("Ex#%d" % h, k), T.Ex[:, w], P[b][:], F.Exp, scale=T.nrate[:])
+    def ages(k, h):
+        b = 6 - 2 * k + h
+        mm(tk("nB Lg#%d" % h, k), "P%d" % b, [(P[b][:], T.nB[:], T.Lg[:, cs_(1024 * k + 512 * h, 512)], False, True)], True)
 
-    def signs(k, part):
-        for h in range(2):
-            b = 6 * k + h
-            if part == "p":
-                reps(b, "wb", k, h, True)
-            else:
-                act("P%d" % b, tk("wr#%d" % h, k), T.wr[:, cs_(1024 * k + 512 * h, 512)], P[b][:])
+    def decay(k, h):
+        b = 6 - 2 * k + h
+        act("P%d nrate" % b, tk("Ex#%d" % h, k), T.Ex[:, cs_(1024 * k + 512 * h, 512)], P[b][:], F.Exp, scale=T.nrate[:])
 
-    def product(k):
-        w = cs_(1024 * k, 1024)
-        tt(tk("V cg# Ex#0 Ex#1", k), tk("prod#", k), T.prod[:, w], T.V[:, 0:S].indirect(T.cg[:, cs_(64 * k, 64)]),
-           T.Ex[:, w], A.mult)
+    def signs(k, h):
+        b = 1 + 5 * k + h
+        act("P%d" % b, tk("wr#%d" % h, k), T.wr[:, cs_(1024 * k + 512 * h, 512)], P[b][:])
 
-    def update(k):
-        w = cs_(1024 * k, 1024)
-        tt(tk("prod# wr#0 wr#1 cs#", k), "V", T.V[:].indirect(T.cs[:, cs_(64 * k, 64)]), T.prod[:, w], T.wr[:, w],
-           A.add)
+    def product(k, h):
+        w = cs_(1024 * k + 512 * h, 512)
+        tt(tk("V cg# Ex#%d" % h, k), tk("prod#%d" % h, k), T.prod[:, w],
+           T.V[:, 0:S].indirect(T.cg[:, cs_(64 * k + 32 * h, 32)]), T.Ex[:, w], A.mult)
 
-    def answers(k, fill, fill2):
-        mine = T.ans[:, cs_(1024 * k + 128 * me, 128)]
-        steps = []
-        for b0, b1, how in CHUNKS[k]:
-            w = slice(1024 * k + 128 * b0, 1024 * k + 128 * b1)
-            t = {n: " ".join("%s%d_%d" % (n, k, j) for j in range(b0, b1)) for n in ("N1", "N3", "N4", "acc", "OUT")}
-            nb = {n: T.V[:, 0:S].indirect(T[n][:, 64 * k + 8 * b0:64 * k + 8 * b1]) for n in ("n1", "n2", "n3", "n4")}
-            out = mine if b1 == 8 else T.OUT[:, w]
-            if how == "p":
-                ps = P[0][:, 0:128 * (b1 - b0)]
-                for j, (buf, n) in enumerate([("N1", "n1"), ("N3", "n3"), ("acc", "n2"), ("N4", "n4")]):
-                    act(tk("V %s#" % n, k), t[buf], T[buf][:, w], nb[n])
-                    mm("idf " + t[buf], "P0", [(ps, T.idf[:], T[buf][:, w], j == 0, j == 3)], True)
-                fill2()
-                act("P0", t["OUT"], out, ps)
-                continue
-            act(tk("V n1#", k), t["N1"], T.N1[:, w], nb["n1"])
-            steps.append([(tk("V n2# ", k) + t["N1"], t["acc"], T.acc[:, w], nb["n2"], T.N1[:, w]),
-                          (tk("V n3# ", k) + t["acc"], t["N3"], T.N3[:, w], nb["n3"], T.acc[:, w]),
-                          (tk("V n4# ", k) + t["N3"], t["OUT"], out, nb["n4"], T.N3[:, w])])
-        fill()
+    def update(k, b0, b1):
+        w = slice(1024 * k + 128 * b0, 1024 * k + 128 * b1)
+        tt(tk("cs# " + " ".join("prod#%d wr#%d" % (h, h) for h in range(b0 // 4, (b1 + 3) // 4)), k), "V",
+           T.V[:].indirect(T.cs[:, 64 * k + 8 * b0:64 * k + 8 * b1]), T.prod[:, w], T.wr[:, w], A.add)
+
+    def chunk(k, b0, b1):
+        w = slice(1024 * k + 128 * b0, 1024 * k + 128 * b1)
+        t = {n: " ".join("%s%d_%d" % (n, k, j) for j in range(b0, b1)) for n in ("N1", "N3", "N4", "acc", "OUT")}
+        nb = {n: T.V[:, 0:S].indirect(T[n][:, 64 * k + 8 * b0:64 * k + 8 * b1]) for n in ("n1", "n2", "n3", "n4")}
+        return w, t, nb
+
+    def mine(k):
+        return T.ans[:, cs_(1024 * k + 128 * me, 128)]
+
+    def summed(k, b0, b1, bank):
+        w, t, nb = chunk(k, b0, b1)
+        ps = P[bank][:, 0:128 * (b1 - b0)]
+        for j, (buf, n) in enumerate([("N1", "n1"), ("N3", "n3"), ("acc", "n2"), ("N4", "n4")]):
+            act(tk("V %s#" % n, k), t[buf], T[buf][:, w], nb[n])
+            mm("idf " + t[buf], "P%d" % bank, [(ps, T.idf[:], T[buf][:, w], j == 0, j == 3)], True)
+        return lambda: act("P%d" % bank, t["OUT"], T.OUT[:, w], ps)
+
+    def first(k, b0, b1):
+        w, t, nb = chunk(k, b0, b1)
+        act(tk("V n1#", k), t["N1"], T.N1[:, w], nb["n1"])
+
+    def rest(k, b0, b1):
+        w, t, nb = chunk(k, b0, b1)
+        out = mine(k) if b0 == 7 else T.OUT[:, w]
+        return [(tk("V n2# ", k) + t["N1"], t["acc"], T.acc[:, w], nb["n2"], T.N1[:, w]),
+                (tk("V n3# ", k) + t["acc"], t["N3"], T.N3[:, w], nb["n3"], T.acc[:, w]),
+                (tk("V n4# ", k) + t["N3"], t["OUT"], out, nb["n4"], T.N3[:, w])]
+
+    def weave(steps):
         seq = steps[0][:-1]
         for i in range(len(steps)):
             nxt = steps[i + 1] if i + 1 < len(steps) else []
@@ -397,20 +449,22 @@ def rank_program(g, core, T, topo):
         for s in seq:
             tt(s[0], s[1], s[2], s[3], s[4], A.add)
 
-        def go(ps, ess):
-            trs = []
-            for p, es in zip(ps, ess):
-                src = T.OUT[:, cs_(1024 * k + 128 * p, 128)]
-                if p < 2:
-                    trs.append(transfer(topo, helper[me][p], es, T.sem[tk("rel#", k)], src, T.rel[:, cs_(128 * k, 128)]))
-                else:
-                    trs.append(transfer(topo, cores[order[me][p]], es, T.sem[tk("ans#", k)], src, mine))
-            send(" ".join("OUT%d_%d" % (k, p) for p in ps), trs, 8)
+    def go(k, ps, ess):
+        trs = []
+        for p, es in zip(ps, ess):
+            src = T.OUT[:, cs_(1024 * k + 128 * p, 128)]
+            if p < 2:
+                trs.append(transfer(topo, helper[me][p], es, T.sem[tk("rel#", k)], src, T.rel[:, cs_(128 * k, 128)]))
+            else:
+                trs.append(transfer(topo, cores[order[me][p]], es, T.sem[tk("ans#", k)], src, mine(k)))
+        send(" ".join("OUT%d_%d" % (k, p) for p in ps), trs, 8)
+
+    def sends(k):
         for p in range(2):
-            go([p], [on if topo.chip(helper[me][p]) == topo.chip(core) else off])
-        go([2, 3], [off[0:4], off[4:8]])
+            go(k, [p], [on if topo.chip(helper[me][p]) == topo.chip(core) else off])
+        go(k, [2, 3], [off[0:4], off[4:8]])
         for ps in ([[4, 5], [6]] if k == 0 else [[6], [4, 5]]):
-            go(ps, [on] if len(ps) == 1 else [on[0:4], on[4:8]])
+            go(k, ps, [on] if len(ps) == 1 else [on[0:4], on[4:8]])
         arrives(tk("ans#", k), tk("ans#", k), 40)
 
     def back(k, f, e0, e1, dq):
@@ -422,23 +476,69 @@ def rank_program(g, core, T, topo):
         dma(dq, tok, "", T.y[:, w], T.Y[:, w])
 
     lists_a(0)
-    op("v", "ti0 t16", "A0", lambda e: [e.tensor_scalar(T.A0[:, r::16], T.ti[:, 0:64], T.t16[:, r:r + 1], None, A.mult)
-                                        for r in range(16)])
-    lists_b(0)
-    cp("A0 cs0", "L", T.L[:].indirect(T.cs[:, 0:64]), T.A0[:])
-    paysend(1, act)
-    decay(0)
-    signs(0, "p")
-    signs(0, "a")
-    product(0)
+    lgather(0, 0)
+    lgather(0, 1)
+    reps(6, "th", 0, 0, False)
+    ages(0, 0)
+    place(1, 1)
+    reps(7, "th", 0, 1, False)
+    words(1)
+    ages(0, 1)
+    lists_w(0)
+    reps(1, "wb", 0, 0, True)
+    reps(2, "wb", 0, 1, True)
+    decay(0, 0)
+    decay(0, 1)
+    signs(0, 0)
+    paysend(1)
+    signs(0, 1)
+    product(0, 0)
+    product(0, 1)
+    update(0, 0, 4)
+    act("t16", "e1", T.e1[:], T.t16[:, 1:2], scale=2048.0)
+    act("ident", "idf", T.idf[:], T.ident[:])
+    for h in range(2):
+        reps(3 * h, "th", 0, h, True)
+        act("P%d t16 e1" % (3 * h), "dts%d" % h, T.dts[:, cs_(512 * h, 512)], P[3 * h][:],
+            scale=T.t16[:, 0:1], bias=T.e1[:])
+    dtinit(1)
+    update(0, 4, 7)
     lists_a(1)
-    update(0)
-    decay(1)
-    lists_b(1)
-    signs(1, "p")
-    answers(0, lambda: product(1), lambda: signs(1, "a"))
-    update(1)
-    answers(1, lambda: None, lambda: None)
+    lists_n()
+    lists_w(1)
+    update(0, 7, 8)
+    reps(4, "th", 1, 0, False)
+    cp("dts0 dts1 cs0", LL, T.L[:].indirect(T.cs[:, 0:64]), T.dts[:])
+    first(0, 3, 8)
+    reps(5, "th", 1, 1, False)
+    out_a = summed(0, 0, 2, 0)
+    out_b = summed(0, 2, 3, 3)
+    out_a()
+    lgather(1, 0)
+    ages(1, 0)
+    lgather(1, 1)
+    ages(1, 1)
+    decay(1, 0)
+    decay(1, 1)
+    reps(6, "wb", 1, 0, True)
+    signs(1, 0)
+    out_b()
+    reps(7, "wb", 1, 1, True)
+    signs(1, 1)
+    weave([rest(0, 3, 7), rest(0, 7, 8)])
+    sends(0)
+    product(1, 0)
+    product(1, 1)
+    update(1, 0, 8)
+    steps = []
+    for b0, b1, how in CHUNKS:
+        if how == "p":
+            summed(1, b0, b1, 0)()
+        else:
+            first(1, b0, b1)
+            steps.append(rest(1, b0, b1))
+    weave(steps)
+    sends(1)
     back(0, cp, 0, 768, "s")
     back(1, cp, 0, 384, "s")
     back(1, act, 384, 768, "a")

@@ -10,10 +10,10 @@ _SB = {
     I32: dict(tm_i=96, pix_i=96, pol_i=96, shI=512, last_i=256, k3=40, k15=40, parI=1, p4I=1, colI=48, hiI=96, loI=96,
               u=96, q=96, cc=192, xi=128, ci=128, ti=128, pi=128),
     F32: dict(rate_s=1, V=WIN, L=WIN, t16=16, tbl=8, t4=16, pcol=1, par=1, p4=1, w1=1, wcol=1, spare=64, spw=64,
-              idf=128, nrate=1, e1=1, lf=256, win=256, candf=768, Zf=144, mask=1536, psend=128, pland=128, Ex=2048, wr=2048,
-              prod=2048, dts=1024, N1=2048, N3=2048, N4=2048, acc=2048, OUT=2048, ans=2048, Y=1536, rel=256),
+              idf=128, nrate=1, e1=1, lf=256, win=256, candf=768, Zf=144, mask=1536, psend=128, pland=128, Ex=2048,
+              wr=2048, prod=2048, dts=1024, N1=2048, N3=2048, N4=2048, acc=2048, OUT=2048, ans=2048, Y=1536, rel=256),
     BF: dict(ones=528, B1=128, B=128, U=128, ident=128, Zb=144, Rep=2048, reset=384, Q=528, J=384, nB=128, C0=128,
-             C1=128, C2=128, hs=256, cand=768, ind=768, scn=768, wb=128, cb=192, tb=288, X=384, dmask=384,
+             C1=128, C2=128, hs=256, cand=768, ind=768, scn=768, wb=128, cb=192, tb=288, X=384, dmask=768,
              gexp=1536, W=2048),
     U16: dict(xU=48, pmU=48, hiU=96, loU=96, slot=96, cg=128, cs=128, n1=128, n2=128, n3=128, n4=128),
     F16: dict(th=128, M=768, Lg=2048)}
@@ -23,7 +23,7 @@ for _b in range(8):
 SEMAPHORES = ["cv", "ca", "cp", "cq", "sent", "pay0", "pay1", "ans0", "ans1", "rel0", "rel1"] + \
              ["d%d" % i for i in range(16)]
 
-CHUNKS = [(0, 1, "v"), (1, 2, "v"), (2, 4, "v"), (6, 7, "v"), (7, 8, "v"), (4, 6, "p")]
+HANDED = {False: (1,), True: (0, 1, 2)}
 
 
 def cs_(a, n):
@@ -39,14 +39,14 @@ def layout(T, topo):
         i = near.index(o)
         order[o] = [far[(i + j) % len(far)] for j in range(len(far))] + \
                    [near[(i + j) % len(near)] for j in range(1, len(near) + 1)]
-        helper[o] = []
-        for j in range(2):
-            d = cores[order[o][j]]
-            cand = [h for h in range(NC) if h not in used and topo.mates(topo.chip(h), topo.chip(d))
-                    and (topo.die(h) == topo.die(co)) == (j == 1) and topo.may_write(co, h) and topo.may_write(h, d)]
-            if not cand:
-                cand = [h for h in topo.cores_of(co) if h not in used and topo.die(h) != topo.die(co)]
-            helper[o].append(cand[0])
+        d = cores[far[0]]
+        over = [h for h in range(NC) if topo.mates(topo.chip(h), topo.chip(d)) and topo.may_write(co, h)
+                and topo.may_write(h, d)]
+        helper[o] = {}
+        for j, b in enumerate(HANDED[bool(over)]):
+            cand = [h for h in over if h not in used and (topo.die(h) == topo.die(co)) == (j == 1) and j < 2] or \
+                   [h for h in topo.cores_of(co) if h not in used and topo.die(h) != topo.die(co)]
+            helper[o][b] = cand[0]
             used.add(cand[0])
     return order, helper
 
@@ -57,10 +57,20 @@ def transfer(topo, d, es, sem, src, dst):
                              remote_sem=sem, src=src, dst=dst)
 
 
-def helper_program(g, core, T, topo, o, d):
+def plan(T, topo, order, helper, o):
+    cores = list(T.cores)
+    off = topo.engines(cores[o], cores[order[o][0]])
+    on = [e for e in topo.engines(cores[o], cores[order[o][4]]) if e not in off]
+    near = [(4, on[0:4]), (5, off), (6, on[4:8])]
+    if 2 in helper[o]:
+        return [[(0, off)], [(1, off)], [(2, on), (3, off)], near]
+    return [[(0, off)], [(1, on)], [(2, off[0:4]), (3, off[4:8])], near]
+
+
+def helper_program(g, core, T, topo, o, d, n):
     es = topo.engines(core, d)
     for k in range(2):
-        g.wait_ge(T.sem["rel%d" % k], 8)
+        g.wait_ge(T.sem["rel%d" % k], n)
         g.remote_dma_fused([transfer(topo, d, es, T.sem["ans%d" % k], T.rel[:, cs_(128 * k, 128)],
                                      T.ans[:, cs_(1024 * k + 128 * o, 128)])], local_sem=T.sem.sent)
     g.wait_ge(T.sem.sent, 2 * len(es))
@@ -72,8 +82,9 @@ def rank_program(g, core, T, topo):
     cores = list(T.cores)
     if me is None:
         for o, hs in helper.items():
-            if core in hs:
-                helper_program(g, core, T, topo, o, cores[order[o][hs.index(core)]])
+            for b in [b for b, h in hs.items() if h == core]:
+                n = [len(es) for call in plan(T, topo, order, helper, o) for p, es in call if p == b]
+                helper_program(g, core, T, topo, o, cores[order[o][b]], n[0])
         return
     Q = {"v": g.vector, "a": g.scalar, "p": g.tensor, "g": g, "s": g.sync}
     CS = {"v": "cv", "a": "ca", "p": "cp", "g": "cq"}
@@ -177,6 +188,9 @@ def rank_program(g, core, T, topo):
     def tk(s, k):
         return s.replace("#", str(k))
 
+    def nothing():
+        pass
+
     P = [T["P%d" % b] for b in range(8)]
     off = topo.engines(core, cores[order[me][0]])
     on = [e for e in topo.engines(core, cores[order[me][4]]) if e not in off]
@@ -210,13 +224,14 @@ def rank_program(g, core, T, topo):
     iota("J", T.J[:], [[128, 8], [0, 48]], 0, 0, **small)
     sel("nB", "U", T.U[:], T.nB[:], dg, A.is_gt, 0, 1)
     sel("ones", "reset", T.reset[:], T.ones[:, 0:384], [[0, 8], [1, 48]], A.is_gt, 0, 0)
+    iota("spare", T.spare[:], [[16, 64]], S, 1, **small)
     iota("W1", T.W[:, 1024:2048], [[0, 1024]], EMPTY, 0, **small)
 
     def repeat(j):
         sel("ones", "Rep%d" % j, T.Rep[:, cs_(512 * j, 512)], T.ones[:, 0:512], [[-1, 4], [-16, 8], [0, 16]],
             A.is_equal, -4 * j, 1)
-    repeat(0)
-    repeat(1)
+    for j in range(3):
+        repeat(j)
     ms("W0", T.W[:, 0:1024], float(EMPTY))
     ts("ka kb kc", "k15", T.k15[:], T.k3[:], 15, AND)
     ts("ka", "parI", T.parI[:], T.k3[:, 0:1], 1, AND)
@@ -225,7 +240,7 @@ def rank_program(g, core, T, topo):
     ts("k15", "t4", T.t4[:], T.k15[:, 24:40], 4.0, A.is_lt)
     ts("k15", "tbl", T.tbl[:], T.k15[:, 16:24], 2.0, A.is_lt)
     ts("colI pcol", "pmU", T.pmU[:], T.colI[:], 0.0, A.mult, T.pcol[:], A.add)
-    act("t4 pmU", "dmask", T.dmask[:], T.t4[:].indirect(T.pmU[:, 0:24]))
+    act("t4 pmU", "dm0", T.dmask[:, 0:384], T.t4[:].indirect(T.pmU[:, 0:24]))
     cp("parI", "par", T.par[:], T.parI[:])
     ts("k15", "t16", T.t16[:], T.k15[:, 0:16], 1.0, A.is_lt)
     ts("p4I", "p4", T.p4[:], T.p4I[:], 48.0, A.mult)
@@ -234,7 +249,6 @@ def rank_program(g, core, T, topo):
     ts("colI p4", "xU", T.xU[:], T.colI[:], T.p4[:], A.add)
     ts("w1", "wcol", T.wcol[:], T.w1[:], 1.0, A.add)
     cp("B", "Zb", T.Zb[:, 15:128:16], T.B[:, 0::16])
-    act("Zb", "Zf", T.Zf[:], T.Zb[:], scale=0.5)
 
     ts("tm", "hiI", T.hiI[:], T.tm_i[:], 8, SHR)
     ts("tm", "loI", T.loI[:], T.tm_i[:], 255, AND)
@@ -242,16 +256,16 @@ def rank_program(g, core, T, topo):
     ts("sh00 sh01 par", "hs", T.hs[:], T.shI[:, 0:256], T.par[:], A.mult)
     cp("loI", "loU", T.loU[:], T.loI[:])
     tt("sh00 sh01 hs", "win", T.win[:], T.shI[:, 0:256], T.hs[:], A.subtract)
+    ts("hiI", "tb0", T.tb[:, 0:96], T.hiI[:], 256.0, A.mult)
 
-    def cand(h):
-        w, R = cs_(384 * (h % 2), 384), " loU mask%d" % h
-        out, window = (T.cand, T.win[:]) if h < 2 else (T.candf, T.shI[:, 256:512])
-        tt(("win" if h < 2 else "sh10 sh11") + R, "cand%d" % h, out[:, w],
-           window.indirect(T.loU[:, cs_(24 * h, 24)]), T.mask[:, cs_(384 * h, 384)], A.mult)
+    def cand(k, h):
+        out, window = (T.candf, T.shI[:, 256:512]) if k else (T.cand, T.win[:])
+        tt(("sh10 sh11" if k else "win") + " loU mask%d" % (2 * k + h), "cand%d%d" % (k, h), out[:, cs_(384 * h, 384)],
+           window.indirect(T.loU[:, cs_(48 * k + 24 * h, 24)]), T.mask[:, cs_(768 * k + 384 * h, 384)], A.mult)
 
     def shifts(k):
         Z, c = (T.Zf, T.candf) if k else (T.Zb, T.cand)
-        mm("Zb Zf cand%d cand%d" % (2 * k, 2 * k + 1), "P0",
+        mm(tk("%s cand#0 cand#1" % Z.name, k), "P0",
            [(P[0][:, 0:48], Z[:, cs_(15 - r, 128)], c[:, r:768:16], r == 0, r == 15) for r in range(16)], False)
 
     def quads(k, R, pieces, last):
@@ -268,37 +282,36 @@ def rank_program(g, core, T, topo):
     def base():
         mm("ident J", "P1", [(P[1][:, 0:384], T.ident[:], T.J[:], True, False)], True)
 
-    def sort(k, fill0, fill1, fill2):
-        w, wi = cs_(48 * k, 48), cs_(384 * k, 384)
-        tt("P0 pix", tk("u#", k), T.u[:, w], P[0][:, 0:48], T.pix_i[:, w], A.add)
-        ts(tk("u#", k), tk("ca#", k), T.cc[:, cs_(96 * k, 48)], T.u[:, w], 0xFC0, AND)
-        ts(tk("u#", k), tk("cc#", k), T.cc[:, cs_(96 * k + 48, 48)], T.u[:, w], 0x3F, AND)
-        ts(tk("u#", k), tk("q#", k), T.q[:, w], T.u[:, w], 12, SHR, 7, AND)
+    def pieces(k):
         cp(tk("ca# cc#", k), tk("cb#", k), T.cb[:, cs_(96 * k, 96)], T.cc[:, cs_(96 * k, 96)])
-        fill0()
         quads(k, tk("cb#", k), [(0, T.cb[:, cs_(96 * k, 48)]), (1, T.cb[:, cs_(96 * k + 48, 48)])], True)
         act("P%d wcol" % (4 + k), tk("X#", k), T.X[:, cs_(192 * k, 192)], P[4 + k][:, 0:192], scale=T.wcol[:])
-        for h in range(2):
-            act(tk("X# xU", k), "gexp%d" % (2 * k + h), T.gexp[:, cs_(768 * k + 384 * h, 384)],
-                T.X[:, cs_(192 * k, 192)].indirect(T.xU[:, cs_(24 * h, 24)]))
-        op("v", tk("q#", k), tk("ind#", k),
-           lambda e: [e.tensor_scalar(T.ind[:, cs_(384 * k + 48 * j, 48)], T.q[:, w], float(j), None, A.is_equal)
-                      for j in range(8)])
-        op("v", tk("reset ind#", k), tk("scn#", k),
+        act(tk("X# xU", k), tk("gexp#", k), T.gexp[:, cs_(768 * k, 768)], T.X[:, cs_(192 * k, 192)].indirect(T.xU[:]))
+
+    def sort(k, fill):
+        w, wi = cs_(48 * k, 48), cs_(384 * k, 384)
+        tt("P0 pix", tk("u#", k), T.u[:, w], P[0][:, 0:48], T.pix_i[:, w], A.add)
+        fill[0]()
+        ts(tk("u#", k), tk("q#", k), T.q[:, w], T.u[:, w], 12, SHR, 7, AND)
+        ts(tk("u#", k), tk("ca#", k), T.cc[:, cs_(96 * k, 48)], T.u[:, w], 0xFC0, AND)
+        ts(tk("u#", k), tk("cc#", k), T.cc[:, cs_(96 * k + 48, 48)], T.u[:, w], 0x3F, AND)
+        for j0, j1 in ((0, 2), (2, 8)):
+            op("v", tk("q#", k), tk("ind#%d" % j0, k),
+               lambda e: [e.tensor_scalar(T.ind[:, cs_(384 * k + 48 * j, 48)], T.q[:, w], float(j), None, A.is_equal)
+                          for j in range(j0, j1)])
+            fill[1 + j0 // 2]()
+        op("v", tk("reset ind#0 ind#2", k), tk("scn#", k),
            lambda e: e.tensor_tensor_scan(T.scn[:, wi], T.reset[:], T.ind[:, wi], 0.0, A.mult, A.add))
-        mm(tk("U ind#", k), "P1", [(P[1][:, 0:384], T.U[:], T.ind[:, wi], False, False)], True)
+        mm(tk("U ind#0 ind#2", k), "P1", [(P[1][:, 0:384], T.U[:], T.ind[:, wi], False, False)], True)
         mm(tk("B scn#", k), "P1", [(P[1][:, 0:384], T.B[:], T.scn[:, wi], False, True)], True)
-        fill1()
-        tt(tk("P1 ind#", k), tk("M#", k), T.M[:, wi], T.ind[:, wi], P[1][:, 0:384], A.mult)
+        fill[3]()
+        tt(tk("P1 ind#0 ind#2", k), tk("M#", k), T.M[:, wi], T.ind[:, wi], P[1][:, 0:384], A.mult)
         mm(tk("ident M#", k), "P2", [(P[2][:, 0:48], T.ident[:], T.M[:, cs_(384 * k + 48 * j, 48)], j == 0, j == 7)
                                      for j in range(8)], False)
-        fill2()
+        fill[4]()
         ts("P2", tk("slot#", k), T.slot[:, w], P[2][:, 0:48], -1.0, A.add)
-
-    def place(k, h):
-        tt("gexp%d" % (2 * k + h) + tk(" dmask slot#", k), tk("W#", k),
-           T.W[:, cs_(1024 * k, 1024)].indirect(T.slot[:, cs_(48 * k + 24 * h, 24)]),
-           T.gexp[:, cs_(768 * k + 384 * h, 384)], T.dmask[:], A.mult)
+        tt(tk("gexp# dmask slot#", k), tk("W#", k), T.W[:, cs_(1024 * k, 1024)].indirect(T.slot[:, w]),
+           T.gexp[:, cs_(768 * k, 768)], T.dmask[:], A.mult)
 
     def words(k):
         mm(tk("Zb W#", k), "P3",
@@ -323,58 +336,64 @@ def rank_program(g, core, T, topo):
             mm(tk("ones C#", k + 1), "P%d" % b, [(P[b][:], T[tk("C#", k + 1)][:], T.ones[:, 0:512], True, False)], True)
 
     def lasts(h0, h1):
-        op("a", "lf t16", " ".join("L%d" % h for h in range(h0, h1)),
+        op("a", "lf0 lf t16", " ".join("L%d" % h for h in range(h0, h1)),
            lambda e: [e.activation(T.L[:, cs_(256 * h, 256)], T.lf[:], F.Identity, scale=T.t16[:, h:h + 1])
                       for h in range(h0, h1)])
 
     for h in range(4):
         act("tbl hiU", "mask%d" % h, T.mask[:, cs_(384 * h, 384)], T.tbl[:].indirect(T.hiU[:, cs_(24 * h, 24)]))
-    cand(0)
-    cand(1)
+    act("dm0", "dmask", T.dmask[:, 384:768], T.dmask[:, 0:384])
+    act("Zb", "Zf", T.Zf[:], T.Zb[:], scale=0.5)
+    cand(0, 0)
+    cand(0, 1)
     shifts(0)
-    ts("hiI", "tb0", T.tb[:, 0:96], T.hiI[:], 256.0, A.mult)
     ts("pol", "tb1", T.tb[:, 96:192], T.pol_i[:], 1024.0, A.mult, 1024.0, A.add)
     cp("loI", "tb2", T.tb[:, 192:288], T.loI[:])
     early(0)
     base()
-    ts("last", "lf", T.lf[:], T.last_i[:], 2048.0, A.add)
-    lasts(0, 2)
-    sort(0, lambda: None, lambda: cand(2), lambda: cand(3))
-    shifts(1)
+    ts("last", "lf0", T.lf[:, 0:192], T.last_i[:, 0:192], 2048.0, A.add)
+
+    def rest_of_lasts():
+        ts("last", "lf", T.lf[:, 192:256], T.last_i[:, 192:256], 2048.0, A.add)
+        lasts(0, 2)
+
+    def last_shifts():
+        cand(1, 1)
+        shifts(1)
+
+    def first_list():
+        paysend(0)
+        pieces(1)
+    sort(0, [rest_of_lasts, nothing, lambda: pieces(0), lambda: cand(1, 0), last_shifts])
+    words(0)
     early(1)
     base()
-    place(0, 0)
-    place(0, 1)
-    words(0)
     lasts(2, 11)
-    sort(1, lambda: paysend(0), lambda: None, lambda: None)
-    iota("C1", T.C1[:], [[0, 128]], 16, 0, **small)
-    iota("spare", T.spare[:], [[16, 64]], S, 1, **small)
-    repeat(2)
+    sort(1, [nothing, first_list, nothing, nothing, nothing])
     repeat(3)
-    iota("C2", T.C2[:], [[0, 128]], 32, 0, **small)
+    act("ones", "C1", T.C1[:], T.ones[:, 0:128], scale=16.0)
     lasts(11, 16)
     act("spare", "spw", T.spw[:], T.spare[:], scale=4096.0)
     act("rate", "nrate", T.nrate[:], T.rate_s[:], scale=-1.0)
     dtinit(0)
-    place(1, 0)
+    words(1)
 
     LL = " ".join("L%d" % h for h in range(16))
     RR = "Rep0 Rep1 Rep2 Rep3 "
 
-    def lists_a(k):
+    def lists(k, names):
         w = cs_(64 * k, 64)
-        tt(tk("pland# pown# spw", k), tk("xi#", k), T.xi[:, w], T.pland[:, w], T.spw[:], A.min)
-        ts(tk("xi#", k), tk("ci#", k), T.ci[:, w], T.xi[:, w], 12, SHR)
-        ts(tk("xi#", k), tk("ti#", k), T.ti[:, w], T.xi[:, w], 2047, AND)
-        ts(tk("ci#", k), tk("cg#", k), T.cg[:, w], T.ci[:, w], float(S - 1), A.min)
-        cp(tk("ti#", k), tk("th#", k), T.th[:, w], T.ti[:, w])
-
-    def lists_w(k):
-        w = cs_(64 * k, 64)
-        ts(tk("xi#", k), tk("pi#", k), T.pi[:, w], T.xi[:, w], 2048, AND)
-        cp(tk("ci#", k), tk("cs#", k), T.cs[:, w], T.ci[:, w])
-        ts(tk("pi#", k), tk("wb#", k), T.wb[:, w], T.pi[:, w], 1.0 / 1024, A.mult, -1.0, A.add)
+        how = dict(
+            xi=lambda: tt(tk("pland# pown# spw", k), tk("xi#", k), T.xi[:, w], T.pland[:, w], T.spw[:], A.min),
+            ci=lambda: ts(tk("xi#", k), tk("ci#", k), T.ci[:, w], T.xi[:, w], 12, SHR),
+            ti=lambda: ts(tk("xi#", k), tk("ti#", k), T.ti[:, w], T.xi[:, w], 2047, AND),
+            pi=lambda: ts(tk("xi#", k), tk("pi#", k), T.pi[:, w], T.xi[:, w], 2048, AND),
+            cg=lambda: ts(tk("ci#", k), tk("cg#", k), T.cg[:, w], T.ci[:, w], float(S - 1), A.min),
+            cs=lambda: cp(tk("ci#", k), tk("cs#", k), T.cs[:, w], T.ci[:, w]),
+            th=lambda: cp(tk("ti#", k), tk("th#", k), T.th[:, w], T.ti[:, w]),
+            wb=lambda: ts(tk("pi#", k), tk("wb#", k), T.wb[:, w], T.pi[:, w], 1.0 / 1024, A.mult, -1.0, A.add))
+        for n in names.split():
+            how[n]()
 
     def lists_n():
         ts("cg0 cg1", "n10 n11", T.n1[:], T.cg[:], -1.0, A.add, 0.0, A.max)
@@ -382,9 +401,10 @@ def rank_program(g, core, T, topo):
         ts("cg0 cg1", "n30 n31", T.n3[:], T.cg[:], -256.0, A.add, 0.0, A.max)
         ts("cg0 cg1", "n40 n41", T.n4[:], T.cg[:], 256.0, A.add, float(S - 1), A.min)
 
-    def lgather(k, h):
-        act(LL + tk(" cg#", k), tk("Lg#%d" % h, k), T.Lg[:, cs_(1024 * k + 512 * h, 512)],
-            T.L[:, 0:S].indirect(T.cg[:, cs_(64 * k + 32 * h, 32)]))
+    def lgather(k, q0, q1, f):
+        f(LL + tk(" cg#", k), " ".join("Lg%d%d" % (k, q) for q in range(q0, q1)),
+          T.Lg[:, 1024 * k + 256 * q0:1024 * k + 256 * q1],
+          T.L[:, 0:S].indirect(T.cg[:, 64 * k + 16 * q0:64 * k + 16 * q1]))
 
     def reps(b, name, k, h, closed):
         mm(RR + tk("%s#" % name, k), "P%d" % b,
@@ -393,7 +413,8 @@ def rank_program(g, core, T, topo):
 
     def ages(k, h):
         b = 6 - 2 * k + h
-        mm(tk("nB Lg#%d" % h, k), "P%d" % b, [(P[b][:], T.nB[:], T.Lg[:, cs_(1024 * k + 512 * h, 512)], False, True)], True)
+        mm(tk("nB Lg#%d Lg#%d" % (2 * h, 2 * h + 1), k), "P%d" % b,
+           [(P[b][:], T.nB[:], T.Lg[:, cs_(1024 * k + 512 * h, 512)], False, True)], True)
 
     def decay(k, h):
         b = 6 - 2 * k + h
@@ -428,11 +449,17 @@ def rank_program(g, core, T, topo):
         for j, (buf, n) in enumerate([("N1", "n1"), ("N3", "n3"), ("acc", "n2"), ("N4", "n4")]):
             act(tk("V %s#" % n, k), t[buf], T[buf][:, w], nb[n])
             mm("idf " + t[buf], "P%d" % bank, [(ps, T.idf[:], T[buf][:, w], j == 0, j == 3)], True)
-        return lambda: act("P%d" % bank, t["OUT"], T.OUT[:, w], ps)
+        def out():
+            n = min(b1, 7) - b0
+            act("P%d" % bank, " ".join("OUT%d_%d" % (k, j) for j in range(b0, b0 + n)),
+                T.OUT[:, cs_(1024 * k + 128 * b0, 128 * n)], P[bank][:, 0:128 * n])
+            if b1 == 8:
+                act("P%d" % bank, "OUT%d_7" % k, mine(k), P[bank][:, cs_(128 * n, 128)])
+        return out
 
-    def first(k, b0, b1):
+    def first(k, b0, b1, f=act):
         w, t, nb = chunk(k, b0, b1)
-        act(tk("V n1#", k), t["N1"], T.N1[:, w], nb["n1"])
+        f(tk("V n1#", k), t["N1"], T.N1[:, w], nb["n1"])
 
     def rest(k, b0, b1):
         w, t, nb = chunk(k, b0, b1)
@@ -441,103 +468,100 @@ def rank_program(g, core, T, topo):
                 (tk("V n3# ", k) + t["acc"], t["N3"], T.N3[:, w], nb["n3"], T.acc[:, w]),
                 (tk("V n4# ", k) + t["N3"], t["OUT"], out, nb["n4"], T.N3[:, w])]
 
-    def weave(steps):
-        seq = steps[0][:-1]
-        for i in range(len(steps)):
-            nxt = steps[i + 1] if i + 1 < len(steps) else []
-            seq += nxt[:1] + steps[i][-1:] + nxt[1:-1]
-        for s in seq:
+    def weave(chunks, turns):
+        at = [0] * len(chunks)
+        for c in turns:
+            s = chunks[c][at[c]]
+            at[c] += 1
             tt(s[0], s[1], s[2], s[3], s[4], A.add)
 
-    def go(k, ps, ess):
-        trs = []
-        for p, es in zip(ps, ess):
-            src = T.OUT[:, cs_(1024 * k + 128 * p, 128)]
-            if p < 2:
-                trs.append(transfer(topo, helper[me][p], es, T.sem[tk("rel#", k)], src, T.rel[:, cs_(128 * k, 128)]))
-            else:
-                trs.append(transfer(topo, cores[order[me][p]], es, T.sem[tk("ans#", k)], src, mine(k)))
-        send(" ".join("OUT%d_%d" % (k, p) for p in ps), trs, 8)
-
     def sends(k):
-        for p in range(2):
-            go(k, [p], [on if topo.chip(helper[me][p]) == topo.chip(core) else off])
-        go(k, [2, 3], [off[0:4], off[4:8]])
-        for ps in ([[4, 5], [6]] if k == 0 else [[6], [4, 5]]):
-            go(k, ps, [on] if len(ps) == 1 else [on[0:4], on[4:8]])
-        arrives(tk("ans#", k), tk("ans#", k), 40)
+        for call in plan(T, topo, order, helper, me):
+            trs = []
+            for p, es in call:
+                src = T.OUT[:, cs_(1024 * k + 128 * p, 128)]
+                if p in helper[me]:
+                    trs.append(transfer(topo, helper[me][p], es, T.sem[tk("rel#", k)], src,
+                                        T.rel[:, cs_(128 * k, 128)]))
+                else:
+                    trs.append(transfer(topo, cores[order[me][p]], es, T.sem[tk("ans#", k)], src, mine(k)))
+            send(" ".join("OUT%d_%d" % (k, p) for p, es in call), trs, sum(len(es) for p, es in call))
+        n = 0
+        for o in range(len(cores)):
+            for call in plan(T, topo, order, helper, o):
+                for p, es in call:
+                    if order[o][p] == me:
+                        n += len(topo.engines(helper[o][p], core)) if p in helper[o] else len(es)
+        arrives(tk("ans#", k), tk("ans#", k), n)
 
     def back(k, f, e0, e1, dq):
         w, tok = slice(768 * k + e0, 768 * k + e1), "Y%d_%d" % (k, e0)
         f(tk("ans# OUT#_7 slot#", k), tok, T.Y[:, w],
           T.ans[:, cs_(1024 * k, 1024)].indirect(T.slot[:, 48 * k + e0 // 16:48 * k + e1 // 16]))
-        if k == 0:
-            wait(dq, ("sent", count["sent"], {}))
         dma(dq, tok, "", T.y[:, w], T.Y[:, w])
 
-    lists_a(0)
-    lgather(0, 0)
-    lgather(0, 1)
+    lists(0, "xi ci ti cg th")
+    lgather(0, 0, 1, act)
+    lgather(0, 2, 3, act)
+    paysend(1)
+    lgather(0, 1, 2, cp)
+    lgather(0, 3, 4, cp)
     reps(6, "th", 0, 0, False)
     ages(0, 0)
-    place(1, 1)
     reps(7, "th", 0, 1, False)
-    words(1)
     ages(0, 1)
-    lists_w(0)
+    lists(0, "pi cs wb")
     reps(1, "wb", 0, 0, True)
     reps(2, "wb", 0, 1, True)
     decay(0, 0)
     decay(0, 1)
     signs(0, 0)
-    paysend(1)
     signs(0, 1)
     product(0, 0)
     product(0, 1)
     update(0, 0, 4)
     act("t16", "e1", T.e1[:], T.t16[:, 1:2], scale=2048.0)
+    act("ones", "C2", T.C2[:], T.ones[:, 0:128], scale=32.0)
     act("ident", "idf", T.idf[:], T.ident[:])
     for h in range(2):
         reps(3 * h, "th", 0, h, True)
         act("P%d t16 e1" % (3 * h), "dts%d" % h, T.dts[:, cs_(512 * h, 512)], P[3 * h][:],
             scale=T.t16[:, 0:1], bias=T.e1[:])
     dtinit(1)
-    update(0, 4, 7)
-    lists_a(1)
+    lists(1, "xi ci ti pi cg th wb cs")
     lists_n()
-    lists_w(1)
-    update(0, 7, 8)
+    update(0, 4, 8)
+    for h in range(2):
+        reps(6 + h, "wb", 1, h, True)
+        signs(1, h)
     reps(4, "th", 1, 0, False)
-    cp("dts0 dts1 cs0", LL, T.L[:].indirect(T.cs[:, 0:64]), T.dts[:])
-    first(0, 3, 8)
     reps(5, "th", 1, 1, False)
-    out_a = summed(0, 0, 2, 0)
-    out_b = summed(0, 2, 3, 3)
+    cp("dts0 dts1 cs0", LL, T.L[:].indirect(T.cs[:, 0:64]), T.dts[:])
+    out_a = summed(0, 0, 1, 0)
+    first(0, 1, 6)
     out_a()
-    lgather(1, 0)
+    lgather(1, 0, 2, act)
     ages(1, 0)
-    lgather(1, 1)
+    lgather(1, 2, 4, act)
     ages(1, 1)
     decay(1, 0)
     decay(1, 1)
-    reps(6, "wb", 1, 0, True)
-    signs(1, 0)
-    out_b()
-    reps(7, "wb", 1, 1, True)
-    signs(1, 1)
-    weave([rest(0, 3, 7), rest(0, 7, 8)])
+    summed(0, 6, 8, 3)()
+    weave([rest(0, 1, 4), rest(0, 4, 6)], [0, 1, 0, 1, 0, 1])
     sends(0)
     product(1, 0)
     product(1, 1)
     update(1, 0, 8)
-    steps = []
-    for b0, b1, how in CHUNKS:
-        if how == "p":
-            summed(1, b0, b1, 0)()
-        else:
-            first(1, b0, b1)
-            steps.append(rest(1, b0, b1))
-    weave(steps)
+    first(1, 0, 1)
+    first(1, 7, 8, cp)
+    first(1, 1, 2)
+    first(1, 3, 4)
+    out_a = summed(1, 2, 3, 0)
+    first(1, 4, 6)
+    out_a()
+    summed(1, 6, 7, 3)()
+    weave([rest(1, 0, 1), rest(1, 1, 2), rest(1, 3, 4), rest(1, 4, 6), rest(1, 7, 8)],
+          [0, 0, 1, 0, 1, 2, 1, 2, 3, 2, 3, 4, 3, 4, 4])
     sends(1)
     back(0, cp, 0, 768, "s")
     back(1, cp, 0, 384, "s")

@@ -8,11 +8,11 @@ WIN = 5248
 I32, F32, BF, U16, F16 = "int32", "float32", "bfloat16", "uint16", "float16"
 _SB = {
     I32: dict(tm_i=96, pix_i=96, pol_i=96, shI=512, last_i=256, k3=40, k15=40, parI=1, p4I=1, colI=48, hiI=96, loI=96,
-              u=96, q=96, cc=192, xi=128, ci=128, ti=128, pi=128),
-    F32: dict(rate_s=1, V=WIN, L=WIN, t16=16, tbl=8, t4=16, pcol=1, par=1, p4=1, w1=1, wcol=1, spare=64, spw=64,
-              idf=128, nrate=1, e1=1, lf=256, win=256, candf=768, Zf=144, mask=1536, psend=128, pland=128, Ex=2048,
-              wr=2048, prod=2048, dts=1024, N1=2048, N3=2048, N4=2048, acc=2048, OUT=2048, ans=2048, Y=1536, rel=256),
-    BF: dict(ones=528, B1=128, B=128, U=128, ident=128, Zb=144, Rep=2048, reset=384, Q=528, J=384, nB=128, C0=128,
+              u=96, q=96, cc=192, xi=240, ci=128, ti=128, cm=128),
+    F32: dict(rate_s=1, V=WIN, L=WIN, t16=16, tbl=8, t4=16, pcol=1, par=1, p4=1, w1=1, wcol=1, spare=64,
+              idf=128, nrate=1, e1=1, lf=256, lf2=512, npar=1, win=256, candf=768, Zf=144, mask=1536, Ex=2048,
+              wr=2048, prod=2048, dts=1024, N1=2048, N3=2048, N4=2048, acc=2048, OUT=2048, ans=2048, Y=1536, rel=384),
+    BF: dict(ones=528, B1=128, B=128, U=128, ident=128, Zb=144, Rep=2048, reset=192, Q=528, J=384, nB=128, C0=128,
              C1=128, C2=128, hs=256, cand=768, ind=768, scn=768, wb=128, cb=192, tb=288, X=384, dmask=768,
              gexp=1536, W=2048),
     U16: dict(xU=48, pmU=48, hiU=96, loU=96, slot=96, cg=128, cs=128, n1=128, n2=128, n3=128, n4=128),
@@ -20,9 +20,11 @@ _SB = {
 SCRATCH = {n: ("sbuf", [128, w], d) for d, ws in _SB.items() for n, w in ws.items()}
 for _b in range(8):
     SCRATCH["P%d" % _b] = ("psum", [128, 512], F32)
-SEMAPHORES = ["cv", "ca", "cp", "cq", "sent", "pay0", "pay1", "ans0", "ans1", "rel0", "rel1"] + \
+SEMAPHORES = ["cv", "ca", "cp", "cq", "sent", "pay0", "pay1", "ans0", "ans1", "rel0", "rel1", "rel2"] + \
              ["d%d" % i for i in range(16)]
 
+TWO = 5
+WHOLE = (1, 2)
 HANDED = {False: (1,), True: (0, 1, 2)}
 
 
@@ -53,27 +55,42 @@ def layout(T, topo):
 
 def transfer(topo, d, es, sem, src, dst):
     a = topo.addr(d)
+    srcs = src if isinstance(src, list) else [src]
     return RemoteDMATransfer(dst_ids=[DstId(rid=a[0], pnc=a[1])], dma_engine_mask=sum(1 << e for e in es),
-                             remote_sem=sem, src=src, dst=dst)
+                             remote_sem=sem, srcs=srcs, dsts=[dst], alu_op=int(len(srcs) > 1))
 
 
-def plan(T, topo, order, helper, o):
+def plan(T, topo, order, helper, o, k):
     cores = list(T.cores)
     off = topo.engines(cores[o], cores[order[o][0]])
     on = [e for e in topo.engines(cores[o], cores[order[o][4]]) if e not in off]
-    near = [(4, on[0:4]), (5, off), (6, on[4:8])]
-    if 2 in helper[o]:
-        return [[(0, off)], [(1, off)], [(2, on), (3, off)], near]
-    return [[(0, off)], [(1, on)], [(2, off[0:4]), (3, off[4:8])], near]
+    second = [(1, off), (2, on)] if 2 in helper[o] else [(1, on), (2, off)]
+    last = [(5, off), (6, on)] if k else [(5, on[0:4]), (6, on[4:8])]
+    return [[(0, off)], second, [(3, off), (4, on)], last]
 
 
-def helper_program(g, core, T, topo, o, d, n):
-    es = topo.engines(core, d)
-    for k in range(2):
-        g.wait_ge(T.sem["rel%d" % k], n)
-        g.remote_dma_fused([transfer(topo, d, es, T.sem["ans%d" % k], T.rel[:, cs_(128 * k, 128)],
-                                     T.ans[:, cs_(1024 * k + 128 * o, 128)])], local_sem=T.sem.sent)
-    g.wait_ge(T.sem.sent, 2 * len(es))
+def handed(helper, o, k):
+    ways = {b: (h, 2 * k) for b, h in helper[o].items()}
+    if k == 0 and 0 in ways:
+        ways[3] = (ways[0][0], 1)
+    elif k == 0:
+        ways = {0: (ways[1][0], 0), 1: (ways[1][0], 1)}
+    return ways
+
+
+def helper_program(g, core, T, topo, order, helper):
+    jobs = sorted((turn, k, o, b) for o in helper for k in range(2)
+                  for b, (h, turn) in handed(helper, o, k).items() if h == core)
+    n = 0
+    for turn, k, o, b in jobs:
+        r = order[o][b]
+        es = topo.engines(core, T.cores[r])
+        g.wait_ge(T.sem["rel%d" % turn], [len(e) for call in plan(T, topo, order, helper, o, k) for p, e in call if p == b][0])
+        g.remote_dma_fused([transfer(topo, T.cores[r], es, T.sem["ans%d" % k], T.rel[:, cs_(128 * turn, 128)],
+                                     T.ans[:, cs_(1024 * k + 128 * ((o - r) % 8), 128)])], local_sem=T.sem.sent)
+        n += len(es)
+    if n:
+        g.wait_ge(T.sem.sent, n)
 
 
 def rank_program(g, core, T, topo):
@@ -81,10 +98,7 @@ def rank_program(g, core, T, topo):
     me = T.rank_of(core)
     cores = list(T.cores)
     if me is None:
-        for o, hs in helper.items():
-            for b in [b for b, h in hs.items() if h == core]:
-                n = [len(es) for call in plan(T, topo, order, helper, o) for p, es in call if p == b]
-                helper_program(g, core, T, topo, o, cores[order[o][b]], n[0])
+        helper_program(g, core, T, topo, order, helper)
         return
     Q = {"v": g.vector, "a": g.scalar, "p": g.tensor, "g": g, "s": g.sync}
     CS = {"v": "cv", "a": "ca", "p": "cp", "g": "cq"}
@@ -195,7 +209,8 @@ def rank_program(g, core, T, topo):
     off = topo.engines(core, cores[order[me][0]])
     on = [e for e in topo.engines(core, cores[order[me][4]]) if e not in off]
     AND, SHR = A.bitwise_and, A.arith_shift_right
-    EMPTY = 2 ** 21
+    RB = (1, 6)
+    EMPTY = 2 ** 20
 
     dma("s", "", "tm", T.tm_i[:], T.tm[:])
     dma("a", "", "sh01", T.shI[1::2, 0:256], T.sh[:, 0:2048])
@@ -223,7 +238,7 @@ def rank_program(g, core, T, topo):
     sel("ones", "Q", T.Q[:], T.ones[:], [[-1, 4], [-4, 33], [256, 4]], A.is_equal, -768, 1)
     iota("J", T.J[:], [[128, 8], [0, 48]], 0, 0, **small)
     sel("nB", "U", T.U[:], T.nB[:], dg, A.is_gt, 0, 1)
-    sel("ones", "reset", T.reset[:], T.ones[:, 0:384], [[0, 8], [1, 48]], A.is_gt, 0, 0)
+    sel("ones", "reset", T.reset[:], T.ones[:, 0:192], [[0, 4], [1, 48]], A.is_gt, 0, 0)
     iota("spare", T.spare[:], [[16, 64]], S, 1, **small)
     iota("W1", T.W[:, 1024:2048], [[0, 1024]], EMPTY, 0, **small)
 
@@ -244,7 +259,7 @@ def rank_program(g, core, T, topo):
     cp("parI", "par", T.par[:], T.parI[:])
     ts("k15", "t16", T.t16[:], T.k15[:, 0:16], 1.0, A.is_lt)
     ts("p4I", "p4", T.p4[:], T.p4I[:], 48.0, A.mult)
-    ts("p4I", "w1", T.w1[:], T.p4I[:], 2.0, A.is_lt, 4095.0, A.mult)
+    ts("p4I", "w1", T.w1[:], T.p4I[:], 2.0, A.is_lt, 2047.0, A.mult)
     ms("Zb", T.Zb[:], 0.0)
     ts("colI p4", "xU", T.xU[:], T.colI[:], T.p4[:], A.add)
     ts("w1", "wcol", T.wcol[:], T.w1[:], 1.0, A.add)
@@ -258,14 +273,18 @@ def rank_program(g, core, T, topo):
     tt("sh00 sh01 hs", "win", T.win[:], T.shI[:, 0:256], T.hs[:], A.subtract)
     ts("hiI", "tb0", T.tb[:, 0:96], T.hiI[:], 256.0, A.mult)
 
-    def cand(k, h):
+    picked = []
+
+    def cand(k, e0, e1):
         out, window = (T.candf, T.shI[:, 256:512]) if k else (T.cand, T.win[:])
-        tt(("sh10 sh11" if k else "win") + " loU mask%d" % (2 * k + h), "cand%d%d" % (k, h), out[:, cs_(384 * h, 384)],
-           window.indirect(T.loU[:, cs_(48 * k + 24 * h, 24)]), T.mask[:, cs_(768 * k + 384 * h, 384)], A.mult)
+        picked.append("cand%d_%d" % (k, e0))
+        tt(("sh10 sh11" if k else "win") + " loU mask%d mask%d" % (2 * k + e0 // 384, 2 * k + (e1 - 1) // 384),
+           picked[-1], out[:, e0:e1], window.indirect(T.loU[:, 48 * k + e0 // 16:48 * k + e1 // 16]),
+           T.mask[:, 768 * k + e0:768 * k + e1], A.mult)
 
     def shifts(k):
         Z, c = (T.Zf, T.candf) if k else (T.Zb, T.cand)
-        mm(tk("%s cand#0 cand#1" % Z.name, k), "P0",
+        mm(" ".join([Z.name] + picked), "P0",
            [(P[0][:, 0:48], Z[:, cs_(15 - r, 128)], c[:, r:768:16], r == 0, r == 15) for r in range(16)], False)
 
     def quads(k, R, pieces, last):
@@ -276,41 +295,64 @@ def rank_program(g, core, T, topo):
 
     def early(k):
         mm("ones C0", "P%d" % (4 + k), [(P[4 + k][:, 0:192], T.C0[:], T.ones[:, 0:192], True, False)], True)
-        quads(k, "tb0 tb1 tb2", [(2, T.tb[:, cs_(48 * k, 48)]), (2, T.tb[:, cs_(96 + 48 * k, 48)]),
+        quads(k, "tb0 tb1 tb2", [(2, T.tb[:, cs_(48 * k, 48)]), (0, T.tb[:, cs_(96 + 48 * k, 48)]),
                                  (3, T.tb[:, cs_(192 + 48 * k, 48)])], False)
 
     def base():
-        mm("ident J", "P1", [(P[1][:, 0:384], T.ident[:], T.J[:], True, False)], True)
+        for h, b in enumerate(RB):
+            mm("ident J", "P%d" % b, [(P[b][:, 0:192], T.ident[:], T.J[:, cs_(192 * h, 192)], True, False)], True)
 
     def pieces(k):
         cp(tk("ca# cc#", k), tk("cb#", k), T.cb[:, cs_(96 * k, 96)], T.cc[:, cs_(96 * k, 96)])
         quads(k, tk("cb#", k), [(0, T.cb[:, cs_(96 * k, 48)]), (1, T.cb[:, cs_(96 * k + 48, 48)])], True)
         act("P%d wcol" % (4 + k), tk("X#", k), T.X[:, cs_(192 * k, 192)], P[4 + k][:, 0:192], scale=T.wcol[:])
-        act(tk("X# xU", k), tk("gexp#", k), T.gexp[:, cs_(768 * k, 768)], T.X[:, cs_(192 * k, 192)].indirect(T.xU[:]))
+        spread(k, 0, E - 192 * k, act)
+
+    def spread(k, e0, e1, f):
+        f(tk("X# xU", k), "gexp%d%d" % (k, e0 > 0), T.gexp[:, 768 * k + e0:768 * k + e1],
+          T.X[:, cs_(192 * k, 192)].indirect(T.xU[:, e0 // 16:e1 // 16]))
 
     def sort(k, fill):
-        w, wi = cs_(48 * k, 48), cs_(384 * k, 384)
+        w = cs_(48 * k, 48)
         tt("P0 pix", tk("u#", k), T.u[:, w], P[0][:, 0:48], T.pix_i[:, w], A.add)
         fill[0]()
         ts(tk("u#", k), tk("q#", k), T.q[:, w], T.u[:, w], 12, SHR, 7, AND)
         ts(tk("u#", k), tk("ca#", k), T.cc[:, cs_(96 * k, 48)], T.u[:, w], 0xFC0, AND)
         ts(tk("u#", k), tk("cc#", k), T.cc[:, cs_(96 * k + 48, 48)], T.u[:, w], 0x3F, AND)
-        for j0, j1 in ((0, 2), (2, 8)):
+        half = [(tk("ind#%d ind#%d" % (4 * h, 4 * h + 2), k), cs_(384 * k + 192 * h, 192), RB[h]) for h in range(2)]
+
+        def marks(j0):
             op("v", tk("q#", k), tk("ind#%d" % j0, k),
-               lambda e: [e.tensor_scalar(T.ind[:, cs_(384 * k + 48 * j, 48)], T.q[:, w], float(j), None, A.is_equal)
-                          for j in range(j0, j1)])
-            fill[1 + j0 // 2]()
-        op("v", tk("reset ind#0 ind#2", k), tk("scn#", k),
-           lambda e: e.tensor_tensor_scan(T.scn[:, wi], T.reset[:], T.ind[:, wi], 0.0, A.mult, A.add))
-        mm(tk("U ind#0 ind#2", k), "P1", [(P[1][:, 0:384], T.U[:], T.ind[:, wi], False, False)], True)
-        mm(tk("B scn#", k), "P1", [(P[1][:, 0:384], T.B[:], T.scn[:, wi], False, True)], True)
+               lambda e: [e.tensor_scalar(T.ind[:, cs_(384 * k + 48 * j, 48)], T.q[:, w], float((me + j) % 8), None,
+                                          A.is_equal) for j in (j0, j0 + 1)])
+
+        def counts(h):
+            R, x, b = half[h]
+            op("v", "reset " + R, tk("scn#%d" % h, k),
+               lambda e: e.tensor_tensor_scan(T.scn[:, x], T.reset[:], T.ind[:, x], 0.0, A.mult, A.add))
+            mm("U " + R, "P%d" % b, [(P[b][:, 0:192], T.U[:], T.ind[:, x], False, False)], True)
+            mm(tk("B scn#%d" % h, k), "P%d" % b, [(P[b][:, 0:192], T.B[:], T.scn[:, x], False, True)], True)
+
+        def picks(h):
+            R, x, b = half[h]
+            tt("P%d " % b + R, tk("M#%d" % h, k), T.M[:, x], T.ind[:, x], P[b][:, 0:192], A.mult)
+            mm(tk("ident M#%d" % h, k), "P2", [(P[2][:, 0:48], T.ident[:], T.M[:, cs_(384 * k + 48 * j, 48)], j == 0,
+                                                j == 7) for j in range(4 * h, 4 * h + 4)], False)
+        marks(0)
+        fill[1]()
+        marks(2)
+        marks(4)
+        counts(0)
+        marks(6)
+        fill[2]()
+        counts(1)
+        picks(0)
         fill[3]()
-        tt(tk("P1 ind#0 ind#2", k), tk("M#", k), T.M[:, wi], T.ind[:, wi], P[1][:, 0:384], A.mult)
-        mm(tk("ident M#", k), "P2", [(P[2][:, 0:48], T.ident[:], T.M[:, cs_(384 * k + 48 * j, 48)], j == 0, j == 7)
-                                     for j in range(8)], False)
+        picks(1)
         fill[4]()
         ts("P2", tk("slot#", k), T.slot[:, w], P[2][:, 0:48], -1.0, A.add)
-        tt(tk("gexp# dmask slot#", k), tk("W#", k), T.W[:, cs_(1024 * k, 1024)].indirect(T.slot[:, w]),
+        fill[5]()
+        tt(tk("gexp#0 gexp#1 dmask slot#", k), tk("W#", k), T.W[:, cs_(1024 * k, 1024)].indirect(T.slot[:, w]),
            T.gexp[:, cs_(768 * k, 768)], T.dmask[:], A.mult)
 
     def words(k):
@@ -319,14 +361,14 @@ def rank_program(g, core, T, topo):
             for r in range(16)], False)
 
     def paysend(k):
-        cp("P3", tk("psend#", k), T.psend[:, cs_(64 * k, 64)], P[3][:, 0:64])
-        act(tk("psend#", k), tk("pown#", k), T.pland[:, cs_(64 * k + 56, 8)], T.psend[:, cs_(64 * k + 8 * me, 8)])
+        cp("P3", tk("psend#", k), T.xi[:, cs_(120 * k + 56, 64)], P[3][:, 0:64])
         trs, n = [], 0
         near = [on[0:2], on[2:4], on[4:6]] if k == 0 else [on[4:8], on[0:2], on[2:4]]
         for j, o in enumerate(order[me][:7]):
             es = off[2 * j:2 * j + 2] if j < 4 else near[j - 4]
-            trs.append(transfer(topo, cores[o], es, T.sem[tk("pay#", k)], T.psend[:, cs_(64 * k + 8 * o, 8)],
-                                T.pland[:, cs_(64 * k + 8 * order[o].index(me), 8)]))
+            trs.append(transfer(topo, cores[o], es, T.sem[tk("pay#", k)],
+                                T.xi[:, cs_(120 * k + 56 + 8 * ((o - me) % 8), 8)],
+                                T.xi[:, cs_(120 * k + 8 * order[o].index(me), 8)]))
             n += len(es)
         send(tk("psend#", k), trs, n)
         arrives(tk("pland#", k), tk("pay#", k), n)
@@ -336,70 +378,74 @@ def rank_program(g, core, T, topo):
             mm(tk("ones C#", k + 1), "P%d" % b, [(P[b][:], T[tk("C#", k + 1)][:], T.ones[:, 0:512], True, False)], True)
 
     def lasts(h0, h1):
-        op("a", "lf0 lf t16", " ".join("L%d" % h for h in range(h0, h1)),
-           lambda e: [e.activation(T.L[:, cs_(256 * h, 256)], T.lf[:], F.Identity, scale=T.t16[:, h:h + 1])
+        if h0 == 0:
+            act("lf0 lf1 npar", "lfa", T.lf2[:, 0:256], T.lf[:], scale=T.npar[:])
+            act("lf0 lf1 par", "lfb", T.lf2[:, 256:512], T.lf[:], scale=T.par[:])
+        op("a", "lfa lfb tbl", " ".join("L%d" % h for h in range(h0, h1)),
+           lambda e: [e.activation(T.L[:, cs_(512 * h, 512)], T.lf2[:], F.Identity, scale=T.tbl[:, h:h + 1])
                       for h in range(h0, h1)])
 
     for h in range(4):
         act("tbl hiU", "mask%d" % h, T.mask[:, cs_(384 * h, 384)], T.tbl[:].indirect(T.hiU[:, cs_(24 * h, 24)]))
     act("dm0", "dmask", T.dmask[:, 384:768], T.dmask[:, 0:384])
     act("Zb", "Zf", T.Zf[:], T.Zb[:], scale=0.5)
-    cand(0, 0)
-    cand(0, 1)
+    act("par", "npar", T.npar[:], T.par[:], scale=-1.0, bias=1.0)
+    act("ones", "C1", T.C1[:], T.ones[:, 0:128], scale=16.0)
+    act("rate", "nrate", T.nrate[:], T.rate_s[:], scale=-1.0)
+    cand(0, 0, 384)
+    cand(0, 384, 768)
     shifts(0)
-    ts("pol", "tb1", T.tb[:, 96:192], T.pol_i[:], 1024.0, A.mult, 1024.0, A.add)
+    ts("pol", "tb1", T.tb[:, 96:192], T.pol_i[:], 2048.0, A.mult, 2048.0, A.add)
     cp("loI", "tb2", T.tb[:, 192:288], T.loI[:])
     early(0)
     base()
-    ts("last", "lf0", T.lf[:, 0:192], T.last_i[:, 0:192], 2048.0, A.add)
+    cand(1, 0, 288)
 
-    def rest_of_lasts():
-        ts("last", "lf", T.lf[:, 192:256], T.last_i[:, 192:256], 2048.0, A.add)
-        lasts(0, 2)
+    def more_shifts():
+        early(1)
+        cand(1, 288, 512)
 
     def last_shifts():
-        cand(1, 1)
+        cand(1, 512, 768)
         shifts(1)
 
-    def first_list():
-        paysend(0)
-        pieces(1)
-    sort(0, [rest_of_lasts, nothing, lambda: pieces(0), lambda: cand(1, 0), last_shifts])
+    def times(h):
+        ts("last", "lf%d" % h, T.lf[:, cs_(128 * h, 128)], T.last_i[:, cs_(128 * h, 128)], 2048.0, A.add)
+
+    sort(0, [lambda: times(0), lambda: pieces(0), nothing, more_shifts, last_shifts, lambda: times(1)])
     words(0)
-    early(1)
     base()
-    lasts(2, 11)
-    sort(1, [nothing, first_list, nothing, nothing, nothing])
+    act("t16", "e1", T.e1[:], T.t16[:, 1:2], scale=2048.0)
+    act("ones", "C2", T.C2[:], T.ones[:, 0:128], scale=32.0)
+    act("ident", "idf", T.idf[:], T.ident[:])
+    lasts(0, 4)
+    sort(1, [nothing, lambda: (paysend(0), pieces(1)), nothing, nothing, lambda: spread(1, E - 192, E, cp), nothing])
     repeat(3)
-    act("ones", "C1", T.C1[:], T.ones[:, 0:128], scale=16.0)
-    lasts(11, 16)
-    act("spare", "spw", T.spw[:], T.spare[:], scale=4096.0)
-    act("rate", "nrate", T.nrate[:], T.rate_s[:], scale=-1.0)
+    lasts(4, 8)
     dtinit(0)
     words(1)
 
-    LL = " ".join("L%d" % h for h in range(16))
+    LL = " ".join("L%d" % h for h in range(8))
     RR = "Rep0 Rep1 Rep2 Rep3 "
 
     def lists(k, names):
-        w = cs_(64 * k, 64)
+        w, x, R = cs_(64 * k, 64), T.xi[:, cs_(120 * k, 64)], tk("pland# psend#", k)
         how = dict(
-            xi=lambda: tt(tk("pland# pown# spw", k), tk("xi#", k), T.xi[:, w], T.pland[:, w], T.spw[:], A.min),
-            ci=lambda: ts(tk("xi#", k), tk("ci#", k), T.ci[:, w], T.xi[:, w], 12, SHR),
-            ti=lambda: ts(tk("xi#", k), tk("ti#", k), T.ti[:, w], T.xi[:, w], 2047, AND),
-            pi=lambda: ts(tk("xi#", k), tk("pi#", k), T.pi[:, w], T.xi[:, w], 2048, AND),
+            ci=lambda: ts(R, tk("ci#", k), T.ci[:, w], x, 11, SHR, 0x2FFF, AND),
+            ti=lambda: ts(R, tk("ti#", k), T.ti[:, w], x, 2047, AND),
             cg=lambda: ts(tk("ci#", k), tk("cg#", k), T.cg[:, w], T.ci[:, w], float(S - 1), A.min),
-            cs=lambda: cp(tk("ci#", k), tk("cs#", k), T.cs[:, w], T.ci[:, w]),
+            cm=lambda: tt(tk("ci# spare", k), tk("cm#", k), T.cm[:, w], T.ci[:, w], T.spare[:], A.min),
+            cs=lambda: cp(tk("cm#", k), tk("cs#", k), T.cs[:, w], T.cm[:, w]),
             th=lambda: cp(tk("ti#", k), tk("th#", k), T.th[:, w], T.ti[:, w]),
-            wb=lambda: ts(tk("pi#", k), tk("wb#", k), T.wb[:, w], T.pi[:, w], 1.0 / 1024, A.mult, -1.0, A.add))
+            wb=lambda: ts(R, tk("wb#", k), T.wb[:, w], x, float(2 ** 23), A.is_ge, 2.0, A.mult))
         for n in names.split():
             how[n]()
 
-    def lists_n():
-        ts("cg0 cg1", "n10 n11", T.n1[:], T.cg[:], -1.0, A.add, 0.0, A.max)
-        ts("cg0 cg1", "n20 n21", T.n2[:], T.cg[:], 1.0, A.add, float(S - 1), A.min)
-        ts("cg0 cg1", "n30 n31", T.n3[:], T.cg[:], -256.0, A.add, 0.0, A.max)
-        ts("cg0 cg1", "n40 n41", T.n4[:], T.cg[:], 256.0, A.add, float(S - 1), A.min)
+    def lists_n(k, names):
+        w = cs_(64 * k, 64)
+        for n in names.split():
+            d = dict(n1=-1.0, n2=1.0, n3=-256.0, n4=256.0)[n]
+            ts(tk("cg#", k), n + str(k), T[n][:, w], T.cg[:, w], d, A.add, *((0.0, A.max) if d < 0 else (S - 1.0, A.min)))
 
     def lgather(k, q0, q1, f):
         f(LL + tk(" cg#", k), " ".join("Lg%d%d" % (k, q) for q in range(q0, q1)),
@@ -422,7 +468,7 @@ def rank_program(g, core, T, topo):
 
     def signs(k, h):
         b = 1 + 5 * k + h
-        act("P%d" % b, tk("wr#%d" % h, k), T.wr[:, cs_(1024 * k + 512 * h, 512)], P[b][:])
+        act("P%d" % b, tk("wr#%d" % h, k), T.wr[:, cs_(1024 * k + 512 * h, 512)], P[b][:], bias=-1.0)
 
     def product(k, h):
         w = cs_(1024 * k + 512 * h, 512)
@@ -434,102 +480,79 @@ def rank_program(g, core, T, topo):
         tt(tk("cs# " + " ".join("prod#%d wr#%d" % (h, h) for h in range(b0 // 4, (b1 + 3) // 4)), k), "V",
            T.V[:].indirect(T.cs[:, 64 * k + 8 * b0:64 * k + 8 * b1]), T.prod[:, w], T.wr[:, w], A.add)
 
-    def chunk(k, b0, b1):
+    def fetch(k, b0, b1, n, out, plus=None):
         w = slice(1024 * k + 128 * b0, 1024 * k + 128 * b1)
-        t = {n: " ".join("%s%d_%d" % (n, k, j) for j in range(b0, b1)) for n in ("N1", "N3", "N4", "acc", "OUT")}
-        nb = {n: T.V[:, 0:S].indirect(T[n][:, 64 * k + 8 * b0:64 * k + 8 * b1]) for n in ("n1", "n2", "n3", "n4")}
-        return w, t, nb
+        t = {x: " ".join("%s%d_%d" % (x, k, j) for j in range(b0, b1)) for x in (out, plus)}
+        nb = T.V[:, 0:S].indirect(T[n][:, 64 * k + 8 * b0:64 * k + 8 * b1])
+        if plus:
+            tt("V %s%d %s" % (n, k, t[plus]), t[out], T[out][:, w], nb, T[plus][:, w], A.add)
+        else:
+            act("V %s%d" % (n, k), t[out], T[out][:, w], nb)
 
-    def mine(k):
-        return T.ans[:, cs_(1024 * k + 128 * me, 128)]
+    def parts(k, b):
+        return ("N1",) if k == 0 and b >= TWO else ("OUT",) if k == 1 and b in WHOLE + (5, 6) else ("OUT", "acc")
 
-    def summed(k, b0, b1, bank):
-        w, t, nb = chunk(k, b0, b1)
-        ps = P[bank][:, 0:128 * (b1 - b0)]
-        for j, (buf, n) in enumerate([("N1", "n1"), ("N3", "n3"), ("acc", "n2"), ("N4", "n4")]):
-            act(tk("V %s#" % n, k), t[buf], T[buf][:, w], nb[n])
-            mm("idf " + t[buf], "P%d" % bank, [(ps, T.idf[:], T[buf][:, w], j == 0, j == 3)], True)
-        def out():
-            n = min(b1, 7) - b0
-            act("P%d" % bank, " ".join("OUT%d_%d" % (k, j) for j in range(b0, b0 + n)),
-                T.OUT[:, cs_(1024 * k + 128 * b0, 128 * n)], P[bank][:, 0:128 * n])
-            if b1 == 8:
-                act("P%d" % bank, "OUT%d_7" % k, mine(k), P[bank][:, cs_(128 * n, 128)])
-        return out
-
-    def first(k, b0, b1, f=act):
-        w, t, nb = chunk(k, b0, b1)
-        f(tk("V n1#", k), t["N1"], T.N1[:, w], nb["n1"])
-
-    def rest(k, b0, b1):
-        w, t, nb = chunk(k, b0, b1)
-        out = mine(k) if b0 == 7 else T.OUT[:, w]
-        return [(tk("V n2# ", k) + t["N1"], t["acc"], T.acc[:, w], nb["n2"], T.N1[:, w]),
-                (tk("V n3# ", k) + t["acc"], t["N3"], T.N3[:, w], nb["n3"], T.acc[:, w]),
-                (tk("V n4# ", k) + t["N3"], t["OUT"], out, nb["n4"], T.N3[:, w])]
-
-    def weave(chunks, turns):
-        at = [0] * len(chunks)
-        for c in turns:
-            s = chunks[c][at[c]]
-            at[c] += 1
-            tt(s[0], s[1], s[2], s[3], s[4], A.add)
+    def mine(k, r=me):
+        return T.ans[:, cs_(1024 * k + 128 * ((me - r) % 8), 128)]
 
     def sends(k):
-        for call in plan(T, topo, order, helper, me):
+        for call in plan(T, topo, order, helper, me, k):
             trs = []
             for p, es in call:
-                src = T.OUT[:, cs_(1024 * k + 128 * p, 128)]
-                if p in helper[me]:
-                    trs.append(transfer(topo, helper[me][p], es, T.sem[tk("rel#", k)], src,
-                                        T.rel[:, cs_(128 * k, 128)]))
+                src = [T[n][:, cs_(1024 * k + 128 * p, 128)] for n in parts(k, p)]
+                if p in handed(helper, me, k):
+                    h, turn = handed(helper, me, k)[p]
+                    trs.append(transfer(topo, h, es, T.sem[tk("rel#", turn)], src, T.rel[:, cs_(128 * turn, 128)]))
                 else:
-                    trs.append(transfer(topo, cores[order[me][p]], es, T.sem[tk("ans#", k)], src, mine(k)))
-            send(" ".join("OUT%d_%d" % (k, p) for p, es in call), trs, sum(len(es) for p, es in call))
+                    trs.append(transfer(topo, cores[order[me][p]], es, T.sem[tk("ans#", k)], src,
+                                        mine(k, order[me][p])))
+            send(" ".join("%s%d_%d" % (n, k, p) for p, es in call for n in parts(k, p)), trs,
+                 sum(len(es) for p, es in call))
         n = 0
         for o in range(len(cores)):
-            for call in plan(T, topo, order, helper, o):
+            for call in plan(T, topo, order, helper, o, k):
                 for p, es in call:
                     if order[o][p] == me:
-                        n += len(topo.engines(helper[o][p], core)) if p in helper[o] else len(es)
+                        ways = handed(helper, o, k)
+                        n += len(topo.engines(ways[p][0], core)) if p in ways else len(es)
         arrives(tk("ans#", k), tk("ans#", k), n)
 
     def back(k, f, e0, e1, dq):
         w, tok = slice(768 * k + e0, 768 * k + e1), "Y%d_%d" % (k, e0)
-        f(tk("ans# OUT#_7 slot#", k), tok, T.Y[:, w],
+        f(tk("ans# own# slot#", k), tok, T.Y[:, w],
           T.ans[:, cs_(1024 * k, 1024)].indirect(T.slot[:, 48 * k + e0 // 16:48 * k + e1 // 16]))
         dma(dq, tok, "", T.y[:, w], T.Y[:, w])
 
-    lists(0, "xi ci ti cg th")
+    lists(0, "ci ti cg th")
     lgather(0, 0, 1, act)
     lgather(0, 2, 3, act)
-    paysend(1)
     lgather(0, 1, 2, cp)
+    paysend(1)
     lgather(0, 3, 4, cp)
     reps(6, "th", 0, 0, False)
     ages(0, 0)
     reps(7, "th", 0, 1, False)
     ages(0, 1)
-    lists(0, "pi cs wb")
+    lists(0, "wb cm")
     reps(1, "wb", 0, 0, True)
     reps(2, "wb", 0, 1, True)
+    lists_n(0, "n1")
+    lists(0, "cs")
+    lists_n(0, "n2 n3")
     decay(0, 0)
     decay(0, 1)
     signs(0, 0)
     signs(0, 1)
     product(0, 0)
     product(0, 1)
+    lists_n(0, "n4")
     update(0, 0, 4)
-    act("t16", "e1", T.e1[:], T.t16[:, 1:2], scale=2048.0)
-    act("ones", "C2", T.C2[:], T.ones[:, 0:128], scale=32.0)
-    act("ident", "idf", T.idf[:], T.ident[:])
     for h in range(2):
         reps(3 * h, "th", 0, h, True)
         act("P%d t16 e1" % (3 * h), "dts%d" % h, T.dts[:, cs_(512 * h, 512)], P[3 * h][:],
             scale=T.t16[:, 0:1], bias=T.e1[:])
     dtinit(1)
-    lists(1, "xi ci ti pi cg th wb cs")
-    lists_n()
+    lists(1, "wb ci ti cm th cg cs")
     update(0, 4, 8)
     for h in range(2):
         reps(6 + h, "wb", 1, h, True)
@@ -537,32 +560,57 @@ def rank_program(g, core, T, topo):
     reps(4, "th", 1, 0, False)
     reps(5, "th", 1, 1, False)
     cp("dts0 dts1 cs0", LL, T.L[:].indirect(T.cs[:, 0:64]), T.dts[:])
-    out_a = summed(0, 0, 1, 0)
-    first(0, 1, 6)
-    out_a()
+    fetch(0, 0, TWO, "n1", "N1")
+    fetch(0, 0, TWO, "n3", "N3")
+    fetch(0, TWO, 8, "n1", "N1")
     lgather(1, 0, 2, act)
     ages(1, 0)
     lgather(1, 2, 4, act)
     ages(1, 1)
     decay(1, 0)
     decay(1, 1)
-    summed(0, 6, 8, 3)()
-    weave([rest(0, 1, 4), rest(0, 4, 6)], [0, 1, 0, 1, 0, 1])
+    fetch(0, TWO, 8, "n3", "N3")
+    fetch(0, TWO, 8, "n4", "OUT")
+    for b0, b1 in ((0, 2), (2, TWO)):
+        fetch(0, b0, b1, "n2", "acc", "N1")
+        fetch(0, b0, b1, "n4", "OUT", "N3")
+    fetch(0, TWO, 8, "n2", "acc", "N1")
+    late = slice(128 * TWO, 1024)
+    for j, n in enumerate(("acc", "N3", "OUT")):
+        mm("idf " + " ".join("%s0_%d" % (n, b) for b in range(TWO, 8)), "P0",
+           [(P[0][:, 0:1024 - 128 * TWO], T.idf[:], T[n][:, late], j == 0, j == 2)], True)
+    act("P0", " ".join("N10_%d" % b for b in range(TWO, 7)), T.N1[:, 128 * TWO:896], P[0][:, 0:896 - 128 * TWO])
+    act("P0", "own0", mine(0), P[0][:, cs_(896 - 128 * TWO, 128)])
     sends(0)
     product(1, 0)
     product(1, 1)
+    lists_n(1, "n1")
     update(1, 0, 8)
-    first(1, 0, 1)
-    first(1, 7, 8, cp)
-    first(1, 1, 2)
-    first(1, 3, 4)
-    out_a = summed(1, 2, 3, 0)
-    first(1, 4, 6)
-    out_a()
-    summed(1, 6, 7, 3)()
-    weave([rest(1, 0, 1), rest(1, 1, 2), rest(1, 3, 4), rest(1, 4, 6), rest(1, 7, 8)],
-          [0, 0, 1, 0, 1, 2, 1, 2, 3, 2, 3, 4, 3, 4, 4])
+    def halves(b0, b1):
+        fetch(1, b0, b1, "n1", "N1")
+        fetch(1, b0, b1, "n3", "N3")
+        fetch(1, b0, b1, "n2", "acc", "N1")
+        fetch(1, b0, b1, "n4", "OUT", "N3")
+    lists_n(1, "n3 n2 n4")
+    halves(0, 1)
+    for step in (("n1", "N1"), ("n2", "acc", "N1"), ("n3", "N3", "acc"), ("n4", "OUT", "N3")):
+        for b in WHOLE:
+            fetch(1, b, b + 1, *step)
+    fetch(1, 3, 6, "n1", "N1")
+    fetch(1, 3, 5, "n3", "N3")
+    fetch(1, 7, 8, "n1", "N1")
+    fetch(1, 3, 6, "n2", "acc", "N1")
+    fetch(1, 3, 5, "n4", "OUT", "N3")
+    for j, (n, x) in enumerate((("n1", "N1"), ("n3", "N3"), ("n2", "acc"), ("n4", "N4"))):
+        fetch(1, 6, 7, n, x)
+        mm("idf %s1_6" % x, "P0", [(P[0][:, 0:128], T.idf[:], T[x][:, 1792:1920], j == 0, j == 3)], True)
+    act("P0", "OUT1_6", T.OUT[:, 1792:1920], P[0][:, 0:128])
+    fetch(1, 5, 6, "n3", "N3", "acc")
+    fetch(1, 7, 8, "n2", "acc", "N1")
+    fetch(1, 5, 6, "n4", "OUT", "N3")
     sends(1)
+    fetch(1, 7, 8, "n3", "N3", "acc")
+    tt("V n41 N31_7", "own1", mine(1), T.V[:, 0:S].indirect(T.n4[:, 120:128]), T.N3[:, 1920:2048], A.add)
     back(0, cp, 0, 768, "s")
     back(1, cp, 0, 384, "s")
     back(1, act, 384, 768, "a")

from concourse.bass import DstId, RemoteDMATransfer
from concourse.mybir import AluOpType as A, ActivationFunctionType as F

NC = 64
E, CAP, S = 768, 128, 4096
WIN = 5248

I32, F32, BF, U16, F16 = "int32", "float32", "bfloat16", "uint16", "float16"
_SB = {
    I32: dict(tm_i=96, pix_i=96, pol_i=96, shI=512, last_i=256, k3=40, k15=40, parI=1, p4I=1, colI=48, hiI=96, loI=96,
              u=96, q=96, cc=192, xi=240, ci=128, ti=128, cm=128),
    F32: dict(rate_s=1, V=WIN, L=WIN, t16=16, tbl=8, t4=16, pcol=1, par=1, p4=1, w1=1, wcol=1, spare=64,
              idf=128, nrate=1, e1=1, lf=256, lf2=512, npar=1, win=256, candf=768, Zf=144, mask=1536, Ex=2048,
              wr=2048, prod=2048, dts=1024, N1=2048, N3=2048, N4=2048, acc=2048, OUT=2048, ans=2048, Y=1536, rel=384),
    BF: dict(ones=528, B1=128, B=128, U=128, ident=128, Zb=144, Rep=2048, reset=192, Q=528, J=384, nB=128, C0=128,
             C1=128, C2=128, hs=256, cand=768, ind=768, scn=768, wb=128, cb=192, tb=288, X=384, dmask=768,
             gexp=1536, W=2048),
    U16: dict(xU=48, pmU=48, hiU=96, loU=96, slot=96, cg=128, cs=128, n1=128, n2=128, n3=128, n4=128),
    F16: dict(th=128, M=768, Lg=2048)}
SCRATCH = {n: ("sbuf", [128, w], d) for d, ws in _SB.items() for n, w in ws.items()}
for _b in range(8):
    SCRATCH["P%d" % _b] = ("psum", [128, 512], F32)
SEMAPHORES = ["cv", "ca", "cp", "cq", "sent", "pay0", "pay1", "ans0", "ans1", "rel0", "rel1", "rel2"] + \
             ["d%d" % i for i in range(16)]

TWO = 5
WHOLE = (1, 2)
HANDED = {False: (1,), True: (0, 1, 2)}


def cs_(a, n):
    return slice(a, a + n)


def layout(T, topo):
    cores = list(T.cores)
    order, helper, used = {}, {}, set(cores)
    for o, co in enumerate(cores):
        near = [r for r, c in enumerate(cores) if topo.chip(c) == topo.chip(co)]
        far = [r for r in range(len(cores)) if r not in near]
        i = near.index(o)
        order[o] = [far[(i + j) % len(far)] for j in range(len(far))] + \
                   [near[(i + j) % len(near)] for j in range(1, len(near) + 1)]
        d = cores[far[0]]
        over = [h for h in range(NC) if topo.mates(topo.chip(h), topo.chip(d)) and topo.may_write(co, h)
                and topo.may_write(h, d)]
        helper[o] = {}
        for j, b in enumerate(HANDED[bool(over)]):
            cand = [h for h in over if h not in used and (topo.die(h) == topo.die(co)) == (j == 1) and j < 2] or \
                   [h for h in topo.cores_of(co) if h not in used and topo.die(h) != topo.die(co)]
            helper[o][b] = cand[0]
            used.add(cand[0])
    return order, helper


def transfer(topo, d, es, sem, src, dst):
    a = topo.addr(d)
    srcs = src if isinstance(src, list) else [src]
    return RemoteDMATransfer(dst_ids=[DstId(rid=a[0], pnc=a[1])], dma_engine_mask=sum(1 << e for e in es),
                             remote_sem=sem, srcs=srcs, dsts=[dst], alu_op=int(len(srcs) > 1))


def plan(T, topo, order, helper, o, k):
    cores = list(T.cores)
    off = topo.engines(cores[o], cores[order[o][0]])
    on = [e for e in topo.engines(cores[o], cores[order[o][4]]) if e not in off]
    second = [(1, off), (2, on)] if 2 in helper[o] else [(1, on), (2, off)]
    last = [(5, off), (6, on)] if k else [(5, on[0:4]), (6, on[4:8])]
    return [[(0, off)], second, [(3, off), (4, on)], last]


def handed(helper, o, k):
    ways = {b: (h, 2 * k) for b, h in helper[o].items()}
    if k == 0 and 0 in ways:
        ways[3] = (ways[0][0], 1)
    elif k == 0:
        ways = {0: (ways[1][0], 0), 1: (ways[1][0], 1)}
    return ways


def helper_program(g, core, T, topo, order, helper):
    jobs = sorted((turn, k, o, b) for o in helper for k in range(2)
                  for b, (h, turn) in handed(helper, o, k).items() if h == core)
    n = 0
    for turn, k, o, b in jobs:
        r = order[o][b]
        es = topo.engines(core, T.cores[r])
        g.wait_ge(T.sem["rel%d" % turn], [len(e) for call in plan(T, topo, order, helper, o, k) for p, e in call if p == b][0])
        g.remote_dma_fused([transfer(topo, T.cores[r], es, T.sem["ans%d" % k], T.rel[:, cs_(128 * turn, 128)],
                                     T.ans[:, cs_(1024 * k + 128 * ((o - r) % 8), 128)])], local_sem=T.sem.sent)
        n += len(es)
    if n:
        g.wait_ge(T.sem.sent, n)


def rank_program(g, core, T, topo):
    order, helper = layout(T, topo)
    me = T.rank_of(core)
    cores = list(T.cores)
    if me is None:
        helper_program(g, core, T, topo, order, helper)
        return
    Q = {"v": g.vector, "a": g.scalar, "p": g.tensor, "g": g, "s": g.sync}
    CS = {"v": "cv", "a": "ca", "p": "cp", "g": "cq"}
    count = {"cv": 0, "ca": 0, "cp": 0, "cq": 0, "sent": 0}
    known = {k: {} for k in Q}
    wrote, readers = {}, {}
    ndma = [0]

    def wait(qn, ev):
        sem, val, clock = ev
        if qn == "p" and sem == "cp":
            return
        kn = known[qn]
        if kn.get(sem, 0) < val:
            Q[qn].wait_ge(T.sem[sem], val)
            kn[sem] = val
        for s2, v2 in clock.items():
            if kn.get(s2, 0) < v2:
                kn[s2] = v2

    def before(qn, R, Wr):
        evs = []
        for t in R:
            evs += wrote.get(t, [])
            if t[0] == "P":
                evs += [e for e in readers.get(t, []) if e[0] != CS.get(qn)]
        for t in Wr:
            evs += wrote.get(t, []) + readers.get(t, [])
        best = {}
        for e in evs:
            if e[0] not in best or best[e[0]][1] < e[1]:
                best[e[0]] = e
        for e in best.values():
            wait(qn, e)

    def after(ev, R, Wr):
        for t in R:
            readers.setdefault(t, []).append(ev)
        for t in Wr:
            wrote[t] = [ev]
            readers[t] = []

    def op(qn, R, Wr, fn):
        R, Wr = R.split(), Wr.split()
        before(qn, R, Wr)
        ins = fn(Q[qn])
        sem = CS[qn]
        for i in (ins if isinstance(ins, list) else [ins]):
            i.then_inc(T.sem[sem], 1)
            count[sem] += 1
        after((sem, count[sem], dict(known[qn])), R, Wr)

    def dma(qn, R, Wr, out, in_):
        R, Wr = R.split(), Wr.split()
        before(qn, R, Wr)
        sem = "d%d" % ndma[0]
        ndma[0] += 1
        Q[qn].dma_start(out, in_).then_inc(T.sem[sem], 16)
        count[sem] = 16
        after((sem, 16, dict(known[qn])), R, Wr)

    def send(R, trs, n):
        before("g", R.split(), [])
        g.remote_dma_fused(trs, local_sem=T.sem.sent)
        count["sent"] += n

    def arrives(tok, sem, n):
        count[sem] = n
        wrote[tok] = [(sem, n, {})]

    def ts(R, Wr, out, in0, s1, o1, s2=None, o2=None):
        if o2 is None:
            op("v", R, Wr, lambda e: e.tensor_scalar(out, in0, s1, None, o1))
        else:
            op("v", R, Wr, lambda e: e.tensor_scalar(out, in0, s1, s2, o1, o2))

    def tt(R, Wr, out, a, b, o):
        op("v", R, Wr, lambda e: e.tensor_tensor(out, a, b, o))

    def cp(R, Wr, out, in_):
        op("v", R, Wr, lambda e: e.tensor_copy(out, in_))

    def ms(Wr, ap, val):
        op("v", "", Wr, lambda e: e.memset(ap, val))

    def act(R, Wr, out, in_, f=F.Identity, **kw):
        op("a", R, Wr, lambda e: e.activation(out, in_, f, **kw))

    def mm(R, Wr, items, each):
        def fn(e):
            ins = [e.matmul(*it) for it in items]
            return ins if each else ins[-1]
        op("p", R, Wr, fn)

    def sel(R, Wr, out, in_, pat, cmp, base, cm):
        op("g", R, Wr, lambda e: e.affine_select(out, in_, pat, cmp, 0.0, base, cm))

    def iota(Wr, out, pat, base, cm, **kw):
        op("g", "", Wr, lambda e: e.iota(out, pat, base, cm, **kw))

    def tk(s, k):
        return s.replace("#", str(k))

    def nothing():
        pass

    P = [T["P%d" % b] for b in range(8)]
    off = topo.engines(core, cores[order[me][0]])
    on = [e for e in topo.engines(core, cores[order[me][4]]) if e not in off]
    AND, SHR = A.bitwise_and, A.arith_shift_right
    RB = (1, 6)
    EMPTY = 2 ** 20

    dma("s", "", "tm", T.tm_i[:], T.tm[:])
    dma("a", "", "sh01", T.shI[1::2, 0:256], T.sh[:, 0:2048])
    dma("s", "", "sh00", T.shI[0::2, 0:256], T.sh[:, 0:2048])
    dma("s", "", "pix", T.pix_i[:], T.pix[:])
    dma("s", "", "pol", T.pol_i[:], T.pol[:])
    dma("s", "", "sh10", T.shI[0::2, 256:512], T.sh[:, 2048:4096])
    dma("s", "", "sh11", T.shI[1::2, 256:512], T.sh[:, 2048:4096])
    dma("s", "", "last", T.last_i[:], T.last[:])
    dma("s", "", "rate", T.rate_s[:], T.rate[:])
    dma("s", "", "V", T.V[:, 0:S], T.v[:])

    small = dict(allow_small_or_imprecise_dtypes=True)
    iota("ka", T.k3[:, 0:16], [[-1, 16]], 16, 1)
    iota("kb", T.k3[:, 16:24], [[-2, 8]], 16, 1)
    iota("kc", T.k3[:, 24:40], [[-4, 4], [0, 4]], 16, 1)
    iota("colI", T.colI[:], [[1, 48]], 0, 0)
    ms("ones", T.ones[:], 1.0)
    lo, hi, dg = [[-16, 8], [0, 16]], [[16, 8], [0, 16]], [[-1, 128]]
    sel("ones", "B1", T.B1[:], T.ones[:, 0:128], lo, A.is_ge, 0, 1)
    sel("B1", "B", T.B[:], T.B1[:], hi, A.is_ge, 15, -1)
    act("ones", "C0", T.C0[:], T.ones[:, 0:128], F.Exp, scale=-200.0)
    act("B", "nB", T.nB[:], T.B[:], scale=-1.0)
    sel("ones", "ident", T.ident[:], T.ones[:, 0:128], dg, A.is_equal, 0, 1)
    sel("ones", "Q", T.Q[:], T.ones[:], [[-1, 4], [-4, 33], [256, 4]], A.is_equal, -768, 1)
    iota("J", T.J[:], [[128, 8], [0, 48]], 0, 0, **small)
    sel("nB", "U", T.U[:], T.nB[:], dg, A.is_gt, 0, 1)
    sel("ones", "reset", T.reset[:], T.ones[:, 0:192], [[0, 4], [1, 48]], A.is_gt, 0, 0)
    iota("spare", T.spare[:], [[16, 64]], S, 1, **small)
    iota("W1", T.W[:, 1024:2048], [[0, 1024]], EMPTY, 0, **small)

    def repeat(j):
        sel("ones", "Rep%d" % j, T.Rep[:, cs_(512 * j, 512)], T.ones[:, 0:512], [[-1, 4], [-16, 8], [0, 16]],
            A.is_equal, -4 * j, 1)
    for j in range(3):
        repeat(j)
    ms("W0", T.W[:, 0:1024], float(EMPTY))
    ts("ka kb kc", "k15", T.k15[:], T.k3[:], 15, AND)
    ts("ka", "parI", T.parI[:], T.k3[:, 0:1], 1, AND)
    ts("ka", "p4I", T.p4I[:], T.k3[:, 0:1], 3, AND)
    cp("k15", "pcol", T.pcol[:], T.k15[:, 0:1])
    ts("k15", "t4", T.t4[:], T.k15[:, 24:40], 4.0, A.is_lt)
    ts("k15", "tbl", T.tbl[:], T.k15[:, 16:24], 2.0, A.is_lt)
    ts("colI pcol", "pmU", T.pmU[:], T.colI[:], 0.0, A.mult, T.pcol[:], A.add)
    act("t4 pmU", "dm0", T.dmask[:, 0:384], T.t4[:].indirect(T.pmU[:, 0:24]))
    cp("parI", "par", T.par[:], T.parI[:])
    ts("k15", "t16", T.t16[:], T.k15[:, 0:16], 1.0, A.is_lt)
    ts("p4I", "p4", T.p4[:], T.p4I[:], 48.0, A.mult)
    ts("p4I", "w1", T.w1[:], T.p4I[:], 2.0, A.is_lt, 2047.0, A.mult)
    ms("Zb", T.Zb[:], 0.0)
    ts("colI p4", "xU", T.xU[:], T.colI[:], T.p4[:], A.add)
    ts("w1", "wcol", T.wcol[:], T.w1[:], 1.0, A.add)
    cp("B", "Zb", T.Zb[:, 15:128:16], T.B[:, 0::16])

    ts("tm", "hiI", T.hiI[:], T.tm_i[:], 8, SHR)
    ts("tm", "loI", T.loI[:], T.tm_i[:], 255, AND)
    cp("hiI", "hiU", T.hiU[:], T.hiI[:])
    ts("sh00 sh01 par", "hs", T.hs[:], T.shI[:, 0:256], T.par[:], A.mult)
    cp("loI", "loU", T.loU[:], T.loI[:])
    tt("sh00 sh01 hs", "win", T.win[:], T.shI[:, 0:256], T.hs[:], A.subtract)
    ts("hiI", "tb0", T.tb[:, 0:96], T.hiI[:], 256.0, A.mult)

    picked = []

    def cand(k, e0, e1):
        out, window = (T.candf, T.shI[:, 256:512]) if k else (T.cand, T.win[:])
        picked.append("cand%d_%d" % (k, e0))
        tt(("sh10 sh11" if k else "win") + " loU mask%d mask%d" % (2 * k + e0 // 384, 2 * k + (e1 - 1) // 384),
           picked[-1], out[:, e0:e1], window.indirect(T.loU[:, 48 * k + e0 // 16:48 * k + e1 // 16]),
           T.mask[:, 768 * k + e0:768 * k + e1], A.mult)

    def shifts(k):
        Z, c = (T.Zf, T.candf) if k else (T.Zb, T.cand)
        mm(" ".join([Z.name] + picked), "P0",
           [(P[0][:, 0:48], Z[:, cs_(15 - r, 128)], c[:, r:768:16], r == 0, r == 15) for r in range(16)], False)

    def quads(k, R, pieces, last):
        items = [(P[4 + k][:, cs_(48 * v, 48)], T.Q[:, cs_(132 * v + 3 - b, 128)], src, False, False)
                 for v in range(4) for b, src in pieces]
        items[-1] = items[-1][:4] + (last,)
        mm("Q " + R, "P%d" % (4 + k), items, False)

    def early(k):
        mm("ones C0", "P%d" % (4 + k), [(P[4 + k][:, 0:192], T.C0[:], T.ones[:, 0:192], True, False)], True)
        quads(k, "tb0 tb1 tb2", [(2, T.tb[:, cs_(48 * k, 48)]), (0, T.tb[:, cs_(96 + 48 * k, 48)]),
                                 (3, T.tb[:, cs_(192 + 48 * k, 48)])], False)

    def base():
        for h, b in enumerate(RB):
            mm("ident J", "P%d" % b, [(P[b][:, 0:192], T.ident[:], T.J[:, cs_(192 * h, 192)], True, False)], True)

    def pieces(k):
        cp(tk("ca# cc#", k), tk("cb#", k), T.cb[:, cs_(96 * k, 96)], T.cc[:, cs_(96 * k, 96)])
        quads(k, tk("cb#", k), [(0, T.cb[:, cs_(96 * k, 48)]), (1, T.cb[:, cs_(96 * k + 48, 48)])], True)
        act("P%d wcol" % (4 + k), tk("X#", k), T.X[:, cs_(192 * k, 192)], P[4 + k][:, 0:192], scale=T.wcol[:])
        spread(k, 0, E - 192 * k, act)

    def spread(k, e0, e1, f):
        f(tk("X# xU", k), "gexp%d%d" % (k, e0 > 0), T.gexp[:, 768 * k + e0:768 * k + e1],
          T.X[:, cs_(192 * k, 192)].indirect(T.xU[:, e0 // 16:e1 // 16]))

    def sort(k, fill):
        w = cs_(48 * k, 48)
        tt("P0 pix", tk("u#", k), T.u[:, w], P[0][:, 0:48], T.pix_i[:, w], A.add)
        fill[0]()
        ts(tk("u#", k), tk("q#", k), T.q[:, w], T.u[:, w], 12, SHR, 7, AND)
        ts(tk("u#", k), tk("ca#", k), T.cc[:, cs_(96 * k, 48)], T.u[:, w], 0xFC0, AND)
        ts(tk("u#", k), tk("cc#", k), T.cc[:, cs_(96 * k + 48, 48)], T.u[:, w], 0x3F, AND)
        half = [(tk("ind#%d ind#%d" % (4 * h, 4 * h + 2), k), cs_(384 * k + 192 * h, 192), RB[h]) for h in range(2)]

        def marks(j0):
            op("v", tk("q#", k), tk("ind#%d" % j0, k),
               lambda e: [e.tensor_scalar(T.ind[:, cs_(384 * k + 48 * j, 48)], T.q[:, w], float((me + j) % 8), None,
                                          A.is_equal) for j in (j0, j0 + 1)])

        def counts(h):
            R, x, b = half[h]
            op("v", "reset " + R, tk("scn#%d" % h, k),
               lambda e: e.tensor_tensor_scan(T.scn[:, x], T.reset[:], T.ind[:, x], 0.0, A.mult, A.add))
            mm("U " + R, "P%d" % b, [(P[b][:, 0:192], T.U[:], T.ind[:, x], False, False)], True)
            mm(tk("B scn#%d" % h, k), "P%d" % b, [(P[b][:, 0:192], T.B[:], T.scn[:, x], False, True)], True)

        def picks(h):
            R, x, b = half[h]
            tt("P%d " % b + R, tk("M#%d" % h, k), T.M[:, x], T.ind[:, x], P[b][:, 0:192], A.mult)
            mm(tk("ident M#%d" % h, k), "P2", [(P[2][:, 0:48], T.ident[:], T.M[:, cs_(384 * k + 48 * j, 48)], j == 0,
                                                j == 7) for j in range(4 * h, 4 * h + 4)], False)
        marks(0)
        fill[1]()
        marks(2)
        marks(4)
        counts(0)
        marks(6)
        fill[2]()
        counts(1)
        picks(0)
        fill[3]()
        picks(1)
        fill[4]()
        ts("P2", tk("slot#", k), T.slot[:, w], P[2][:, 0:48], -1.0, A.add)
        fill[5]()
        tt(tk("gexp#0 gexp#1 dmask slot#", k), tk("W#", k), T.W[:, cs_(1024 * k, 1024)].indirect(T.slot[:, w]),
           T.gexp[:, cs_(768 * k, 768)], T.dmask[:], A.mult)

    def words(k):
        mm(tk("Zb W#", k), "P3",
           [(P[3][:, 0:64], T.Zb[:, cs_(15 - r, 128)], T.W[:, 1024 * k + r:1024 * k + 1024:16], r == 0, r == 15)
            for r in range(16)], False)

    def paysend(k):
        cp("P3", tk("psend#", k), T.xi[:, cs_(120 * k + 56, 64)], P[3][:, 0:64])
        trs, n = [], 0
        near = [on[0:2], on[2:4], on[4:6]] if k == 0 else [on[4:8], on[0:2], on[2:4]]
        for j, o in enumerate(order[me][:7]):
            es = off[2 * j:2 * j + 2] if j < 4 else near[j - 4]
            trs.append(transfer(topo, cores[o], es, T.sem[tk("pay#", k)],
                                T.xi[:, cs_(120 * k + 56 + 8 * ((o - me) % 8), 8)],
                                T.xi[:, cs_(120 * k + 8 * order[o].index(me), 8)]))
            n += len(es)
        send(tk("psend#", k), trs, n)
        arrives(tk("pland#", k), tk("pay#", k), n)

    def dtinit(k):
        for b in (6 - 2 * k, 7 - 2 * k):
            mm(tk("ones C#", k + 1), "P%d" % b, [(P[b][:], T[tk("C#", k + 1)][:], T.ones[:, 0:512], True, False)], True)

    def lasts(h0, h1):
        if h0 == 0:
            act("lf0 lf1 npar", "lfa", T.lf2[:, 0:256], T.lf[:], scale=T.npar[:])
            act("lf0 lf1 par", "lfb", T.lf2[:, 256:512], T.lf[:], scale=T.par[:])
        op("a", "lfa lfb tbl", " ".join("L%d" % h for h in range(h0, h1)),
           lambda e: [e.activation(T.L[:, cs_(512 * h, 512)], T.lf2[:], F.Identity, scale=T.tbl[:, h:h + 1])
                      for h in range(h0, h1)])

    for h in range(4):
        act("tbl hiU", "mask%d" % h, T.mask[:, cs_(384 * h, 384)], T.tbl[:].indirect(T.hiU[:, cs_(24 * h, 24)]))
    act("dm0", "dmask", T.dmask[:, 384:768], T.dmask[:, 0:384])
    act("Zb", "Zf", T.Zf[:], T.Zb[:], scale=0.5)
    act("par", "npar", T.npar[:], T.par[:], scale=-1.0, bias=1.0)
    act("ones", "C1", T.C1[:], T.ones[:, 0:128], scale=16.0)
    act("rate", "nrate", T.nrate[:], T.rate_s[:], scale=-1.0)
    cand(0, 0, 384)
    cand(0, 384, 768)
    shifts(0)
    ts("pol", "tb1", T.tb[:, 96:192], T.pol_i[:], 2048.0, A.mult, 2048.0, A.add)
    cp("loI", "tb2", T.tb[:, 192:288], T.loI[:])
    early(0)
    base()
    cand(1, 0, 288)

    def more_shifts():
        early(1)
        cand(1, 288, 512)

    def last_shifts():
        cand(1, 512, 768)
        shifts(1)

    def times(h):
        ts("last", "lf%d" % h, T.lf[:, cs_(128 * h, 128)], T.last_i[:, cs_(128 * h, 128)], 2048.0, A.add)

    sort(0, [lambda: times(0), lambda: pieces(0), nothing, more_shifts, last_shifts, lambda: times(1)])
    words(0)
    base()
    act("t16", "e1", T.e1[:], T.t16[:, 1:2], scale=2048.0)
    act("ones", "C2", T.C2[:], T.ones[:, 0:128], scale=32.0)
    act("ident", "idf", T.idf[:], T.ident[:])
    lasts(0, 4)
    sort(1, [nothing, lambda: (paysend(0), pieces(1)), nothing, nothing, lambda: spread(1, E - 192, E, cp), nothing])
    repeat(3)
    lasts(4, 8)
    dtinit(0)
    words(1)

    LL = " ".join("L%d" % h for h in range(8))
    RR = "Rep0 Rep1 Rep2 Rep3 "

    def lists(k, names):
        w, x, R = cs_(64 * k, 64), T.xi[:, cs_(120 * k, 64)], tk("pland# psend#", k)
        how = dict(
            ci=lambda: ts(R, tk("ci#", k), T.ci[:, w], x, 11, SHR, 0x2FFF, AND),
            ti=lambda: ts(R, tk("ti#", k), T.ti[:, w], x, 2047, AND),
            cg=lambda: ts(tk("ci#", k), tk("cg#", k), T.cg[:, w], T.ci[:, w], float(S - 1), A.min),
            cm=lambda: tt(tk("ci# spare", k), tk("cm#", k), T.cm[:, w], T.ci[:, w], T.spare[:], A.min),
            cs=lambda: cp(tk("cm#", k), tk("cs#", k), T.cs[:, w], T.cm[:, w]),
            th=lambda: cp(tk("ti#", k), tk("th#", k), T.th[:, w], T.ti[:, w]),
            wb=lambda: ts(R, tk("wb#", k), T.wb[:, w], x, float(2 ** 23), A.is_ge, 2.0, A.mult))
        for n in names.split():
            how[n]()

    def lists_n(k, names):
        w = cs_(64 * k, 64)
        for n in names.split():
            d = dict(n1=-1.0, n2=1.0, n3=-256.0, n4=256.0)[n]
            ts(tk("cg#", k), n + str(k), T[n][:, w], T.cg[:, w], d, A.add, *((0.0, A.max) if d < 0 else (S - 1.0, A.min)))

    def lgather(k, q0, q1, f):
        f(LL + tk(" cg#", k), " ".join("Lg%d%d" % (k, q) for q in range(q0, q1)),
          T.Lg[:, 1024 * k + 256 * q0:1024 * k + 256 * q1],
          T.L[:, 0:S].indirect(T.cg[:, 64 * k + 16 * q0:64 * k + 16 * q1]))

    def reps(b, name, k, h, closed):
        mm(RR + tk("%s#" % name, k), "P%d" % b,
           [(P[b][:, r::16], T.Rep[:, cs_(128 * r, 128)], T[name][:, cs_(64 * k + 32 * h, 32)], closed, closed)
            for r in range(16)], True)

    def ages(k, h):
        b = 6 - 2 * k + h
        mm(tk("nB Lg#%d Lg#%d" % (2 * h, 2 * h + 1), k), "P%d" % b,
           [(P[b][:], T.nB[:], T.Lg[:, cs_(1024 * k + 512 * h, 512)], False, True)], True)

    def decay(k, h):
        b = 6 - 2 * k + h
        act("P%d nrate" % b, tk("Ex#%d" % h, k), T.Ex[:, cs_(1024 * k + 512 * h, 512)], P[b][:], F.Exp, scale=T.nrate[:])

    def signs(k, h):
        b = 1 + 5 * k + h
        act("P%d" % b, tk("wr#%d" % h, k), T.wr[:, cs_(1024 * k + 512 * h, 512)], P[b][:], bias=-1.0)

    def product(k, h):
        w = cs_(1024 * k + 512 * h, 512)
        tt(tk("V cg# Ex#%d" % h, k), tk("prod#%d" % h, k), T.prod[:, w],
           T.V[:, 0:S].indirect(T.cg[:, cs_(64 * k + 32 * h, 32)]), T.Ex[:, w], A.mult)

    def update(k, b0, b1):
        w = slice(1024 * k + 128 * b0, 1024 * k + 128 * b1)
        tt(tk("cs# " + " ".join("prod#%d wr#%d" % (h, h) for h in range(b0 // 4, (b1 + 3) // 4)), k), "V",
           T.V[:].indirect(T.cs[:, 64 * k + 8 * b0:64 * k + 8 * b1]), T.prod[:, w], T.wr[:, w], A.add)

    def fetch(k, b0, b1, n, out, plus=None):
        w = slice(1024 * k + 128 * b0, 1024 * k + 128 * b1)
        t = {x: " ".join("%s%d_%d" % (x, k, j) for j in range(b0, b1)) for x in (out, plus)}
        nb = T.V[:, 0:S].indirect(T[n][:, 64 * k + 8 * b0:64 * k + 8 * b1])
        if plus:
            tt("V %s%d %s" % (n, k, t[plus]), t[out], T[out][:, w], nb, T[plus][:, w], A.add)
        else:
            act("V %s%d" % (n, k), t[out], T[out][:, w], nb)

    def parts(k, b):
        return ("N1",) if k == 0 and b >= TWO else ("OUT",) if k == 1 and b in WHOLE + (5, 6) else ("OUT", "acc")

    def mine(k, r=me):
        return T.ans[:, cs_(1024 * k + 128 * ((me - r) % 8), 128)]

    def sends(k):
        for call in plan(T, topo, order, helper, me, k):
            trs = []
            for p, es in call:
                src = [T[n][:, cs_(1024 * k + 128 * p, 128)] for n in parts(k, p)]
                if p in handed(helper, me, k):
                    h, turn = handed(helper, me, k)[p]
                    trs.append(transfer(topo, h, es, T.sem[tk("rel#", turn)], src, T.rel[:, cs_(128 * turn, 128)]))
                else:
                    trs.append(transfer(topo, cores[order[me][p]], es, T.sem[tk("ans#", k)], src,
                                        mine(k, order[me][p])))
            send(" ".join("%s%d_%d" % (n, k, p) for p, es in call for n in parts(k, p)), trs,
                 sum(len(es) for p, es in call))
        n = 0
        for o in range(len(cores)):
            for call in plan(T, topo, order, helper, o, k):
                for p, es in call:
                    if order[o][p] == me:
                        ways = handed(helper, o, k)
                        n += len(topo.engines(ways[p][0], core)) if p in ways else len(es)
        arrives(tk("ans#", k), tk("ans#", k), n)

    def back(k, f, e0, e1, dq):
        w, tok = slice(768 * k + e0, 768 * k + e1), "Y%d_%d" % (k, e0)
        f(tk("ans# own# slot#", k), tok, T.Y[:, w],
          T.ans[:, cs_(1024 * k, 1024)].indirect(T.slot[:, 48 * k + e0 // 16:48 * k + e1 // 16]))
        dma(dq, tok, "", T.y[:, w], T.Y[:, w])

    lists(0, "ci ti cg th")
    lgather(0, 0, 1, act)
    lgather(0, 2, 3, act)
    lgather(0, 1, 2, cp)
    paysend(1)
    lgather(0, 3, 4, cp)
    reps(6, "th", 0, 0, False)
    ages(0, 0)
    reps(7, "th", 0, 1, False)
    ages(0, 1)
    lists(0, "wb cm")
    reps(1, "wb", 0, 0, True)
    reps(2, "wb", 0, 1, True)
    lists_n(0, "n1")
    lists(0, "cs")
    lists_n(0, "n2 n3")
    decay(0, 0)
    decay(0, 1)
    signs(0, 0)
    signs(0, 1)
    product(0, 0)
    product(0, 1)
    lists_n(0, "n4")
    update(0, 0, 4)
    for h in range(2):
        reps(3 * h, "th", 0, h, True)
        act("P%d t16 e1" % (3 * h), "dts%d" % h, T.dts[:, cs_(512 * h, 512)], P[3 * h][:],
            scale=T.t16[:, 0:1], bias=T.e1[:])
    dtinit(1)
    lists(1, "wb ci ti cm th cg cs")
    update(0, 4, 8)
    for h in range(2):
        reps(6 + h, "wb", 1, h, True)
        signs(1, h)
    reps(4, "th", 1, 0, False)
    reps(5, "th", 1, 1, False)
    cp("dts0 dts1 cs0", LL, T.L[:].indirect(T.cs[:, 0:64]), T.dts[:])
    fetch(0, 0, TWO, "n1", "N1")
    fetch(0, 0, TWO, "n3", "N3")
    fetch(0, TWO, 8, "n1", "N1")
    lgather(1, 0, 2, act)
    ages(1, 0)
    lgather(1, 2, 4, act)
    ages(1, 1)
    decay(1, 0)
    decay(1, 1)
    fetch(0, TWO, 8, "n3", "N3")
    fetch(0, TWO, 8, "n4", "OUT")
    for b0, b1 in ((0, 2), (2, TWO)):
        fetch(0, b0, b1, "n2", "acc", "N1")
        fetch(0, b0, b1, "n4", "OUT", "N3")
    fetch(0, TWO, 8, "n2", "acc", "N1")
    late = slice(128 * TWO, 1024)
    for j, n in enumerate(("acc", "N3", "OUT")):
        mm("idf " + " ".join("%s0_%d" % (n, b) for b in range(TWO, 8)), "P0",
           [(P[0][:, 0:1024 - 128 * TWO], T.idf[:], T[n][:, late], j == 0, j == 2)], True)
    act("P0", " ".join("N10_%d" % b for b in range(TWO, 7)), T.N1[:, 128 * TWO:896], P[0][:, 0:896 - 128 * TWO])
    act("P0", "own0", mine(0), P[0][:, cs_(896 - 128 * TWO, 128)])
    sends(0)
    product(1, 0)
    product(1, 1)
    lists_n(1, "n1")
    update(1, 0, 8)
    def halves(b0, b1):
        fetch(1, b0, b1, "n1", "N1")
        fetch(1, b0, b1, "n3", "N3")
        fetch(1, b0, b1, "n2", "acc", "N1")
        fetch(1, b0, b1, "n4", "OUT", "N3")
    lists_n(1, "n3 n2 n4")
    halves(0, 1)
    for step in (("n1", "N1"), ("n2", "acc", "N1"), ("n3", "N3", "acc"), ("n4", "OUT", "N3")):
        for b in WHOLE:
            fetch(1, b, b + 1, *step)
    fetch(1, 3, 6, "n1", "N1")
    fetch(1, 3, 5, "n3", "N3")
    fetch(1, 7, 8, "n1", "N1")
    fetch(1, 3, 6, "n2", "acc", "N1")
    fetch(1, 3, 5, "n4", "OUT", "N3")
    for j, (n, x) in enumerate((("n1", "N1"), ("n3", "N3"), ("n2", "acc"), ("n4", "N4"))):
        fetch(1, 6, 7, n, x)
        mm("idf %s1_6" % x, "P0", [(P[0][:, 0:128], T.idf[:], T[x][:, 1792:1920], j == 0, j == 3)], True)
    act("P0", "OUT1_6", T.OUT[:, 1792:1920], P[0][:, 0:128])
    fetch(1, 5, 6, "n3", "N3", "acc")
    fetch(1, 7, 8, "n2", "acc", "N1")
    fetch(1, 5, 6, "n4", "OUT", "N3")
    sends(1)
    fetch(1, 7, 8, "n3", "N3", "acc")
    tt("V n41 N31_7", "own1", mine(1), T.V[:, 0:S].indirect(T.n4[:, 120:128]), T.N3[:, 1920:2048], A.add)
    back(0, cp, 0, 768, "s")
    back(1, cp, 0, 384, "s")
    back(1, act, 384, 768, "a")
    for sem, n in count.items():
        g.wait_ge(T.sem[sem], n)
